import numpy as np
import ml_dtypes


def mxq(x, axis, fmt="e4m3"):
    dtype, down = {"e4m3": (ml_dtypes.float8_e4m3fn, 7), "e5m2": (ml_dtypes.float8_e5m2, 14)}[fmt]
    v = np.moveaxis(np.asarray(x, np.float32).astype(ml_dtypes.bfloat16).astype(np.float64), axis, -1)
    blocks = v.reshape(v.shape[:-1] + (-1, 32))
    amax = np.abs(blocks).max(-1, keepdims=True)
    byte = np.maximum(np.where(amax > 0, np.frexp(amax)[1] - 1 + 127, 0) - down, 1)
    scale = np.exp2(byte - 127.0)
    codes = (blocks / scale).astype(np.float32).astype(dtype).astype(np.float64)
    return np.moveaxis((codes * scale).reshape(v.shape), -1, axis)


WIDE = False


def mx_kscale(k):
    if not WIDE:
        return np.ones(k)
    levels = np.array([10, -10, 5, -5, 0])
    if k % 512:
        return np.exp2(np.random.permutation(np.resize(levels, k // 32))).repeat(32)
    a = np.empty((k // 512, 16))
    for p in range(k // 512):
        a[p, :8] = np.random.permutation(np.resize(levels, 8))
        for g in range(8):
            far = levels[np.abs(levels - a[p, g]) >= 10]
            a[p, g + 8] = far[np.random.randint(len(far))]
    return np.exp2(a.ravel()).repeat(32)


def f64(x):
    return np.asarray(x).astype(np.float64)


def striped(idx):
    return np.tile(idx.reshape(-1, 16).T, (8, 1)).astype(np.uint16)


def unstriped(offs):
    return offs[:16].T.reshape(-1).astype(np.int64)


def pack_weight(w):
    k, n = w.shape
    w = f64(np.asarray(w, np.float32).astype(ml_dtypes.bfloat16)).reshape(k // 32, 32, n)
    amax = np.abs(w).max(1)
    byte = np.clip(np.where(amax > 0, np.frexp(amax)[1] - 1 + 127 - 7, 1), 1, 254)
    scaled = (w * np.exp2(127.0 - byte)[:, None, :]).reshape(k, n).astype(np.float32)
    words = np.ascontiguousarray(scaled.reshape(k // 512, 128, 4, n).transpose(0, 1, 3, 2)).astype(ml_dtypes.float8_e4m3fn).view(np.uint8)
    return words, np.ascontiguousarray(byte.astype(np.uint8).reshape(k // 512, 16, n))


def unpack_weight(words, scales):
    g, p, n, _ = words.shape
    vals = np.ascontiguousarray(words).view(ml_dtypes.float8_e4m3fn).astype(np.float64) * np.repeat(np.exp2(scales.astype(np.float64) - 127.0), 8, axis=1)[..., None]
    return vals.transpose(0, 1, 3, 2).reshape(g * 512, n)


def relu(v):
    return np.maximum(v, 0.0)


K, T, S, H, N = 512, 2048, 1024, 512, 128


def setup_inputs():
    n = np.random.standard_normal
    s = mx_kscale(K)[:, None]
    u = mx_kscale(H)
    packed_xT = pack_weight(n((K, T)) * s)
    return {
        "x_words": packed_xT[0],
        "x_scales": packed_xT[1],
        "w1": (n((K, H)) / np.sqrt(K) / s * u).astype(np.float32),
        "r1": (n((K, H)) / np.sqrt(K) / s * u).astype(np.float32),
        "w2": (n((H, N)) / np.sqrt(H) / u[:, None]).astype(np.float32),
        "r2": (n((H, N)) / np.sqrt(H) / u[:, None]).astype(np.float32),
        "offs": striped(np.random.permutation(T)[:S]),
    }


def reference(x_words, x_scales, w1, r1, w2, r2, offs):
    xq = unpack_weight(x_words, x_scales)[:, unstriped(offs)]
    h = relu(mxq(f64(w1), 0, "e4m3").T @ xq)
    gg = relu(mxq(f64(r1), 0, "e4m3").T @ xq)
    y = mxq(f64(r2), 0, "e4m3").T @ mxq(gg, 0, "e4m3")
    dd = (mxq(f64(w2), 0, "e4m3").T @ mxq(h, 0, "e4m3")) - y
    return dd * dd

@@ -1,0 +1,121 @@
+from contextlib import ExitStack
+
+import concourse.mybir as mybir
+
+K, T, S, H, N = 512, 2048, 1024, 512, 128
+FLOPS = 2 * 2 * S * (K * H + H * N)
+
+F32 = mybir.dt.float32
+BF16 = mybir.dt.bfloat16
+I32 = mybir.dt.int32
+U32 = mybir.dt.uint32
+U16 = mybir.dt.uint16
+U8 = mybir.dt.uint8
+FP8X4 = mybir.dt.float8_e4m3fn_x4
+ACT = mybir.ActivationFunctionType
+
+P = 128
+PACK = 4
+GATHER = 256
+BANK = 128
+PAIR = 256
+HALF = H // 2
+H_VECTOR_BANKS = ()
+G_VECTOR_BANKS = (1, 3, 5, 7)
+
+
+def tile_picked_yrnd_sq_p_kernel(tc, x_words, x_scales, w1, r1, w2, r2, offs, out):
+    nc = tc.nc
+    with ExitStack() as ctx:
+        keep = ctx.enter_context(tc.tile_pool(name="keep", bufs=1))
+        hidden_psum = ctx.enter_context(tc.psum_pool(name="hidden_psum", bufs=6))
+        diff_psum = ctx.enter_context(tc.psum_pool(name="diff_psum", bufs=2))
+
+        offsets = keep.tile([P, S // 16], U16, name="offsets")
+        nc.sync.dma_start(offsets[:], offs)
+
+        scale_table = keep.tile([P, T], U8, name="scale_table", align_bytes=64)
+        nc.vector.memset(scale_table[:].bitcast(I32), 0)
+        word_table = keep.tile([P, T], I32, name="word_table", align_bytes=64)
+        nc.sync.dma_start(out=word_table[:], in_=x_words[0].rearrange("p n t -> p (n t)").bitcast(I32))
+        for q in range(4):
+            nc.sync.dma_start(out=scale_table[32 * q : 32 * q + 4, :].bitcast(I32), in_=x_scales[0, 4 * q : 4 * q + 4, :].bitcast(I32))
+
+        warm = keep.tile([P, 1], F32, name="warm", tag="raw")
+        nc.gpsimd.memset(warm[:], 0.0)
+        warm_out = keep.tile([P, 1], F32, name="warm_out")
+        nc.scalar.activation(warm_out[:], warm[:], ACT.Relu)
+
+        raw = keep.tile([P, PACK * (2 * H + 2 * N)], F32, name="raw", tag="raw")
+
+        def load(w, cols, place):
+            width = cols.stop - cols.start
+            rows = raw[:, PACK * place : PACK * (place + width)].rearrange("p (j c) -> p j c", j=PACK)
+            nc.sync.dma_start(out=rows, in_=w.rearrange("(p j) c -> p j c", j=PACK)[:, :, cols])
+            return rows
+
+        halves = [slice(0, HALF), slice(HALF, H)]
+        w1_raw = [load(w1, cols, cols.start) for cols in halves]
+        w2_raw = load(w2, slice(0, N), H)
+        r2_raw = load(r2, slice(0, N), H + N)
+        r1_raw = [load(r1, cols, H + 2 * N + cols.start) for cols in halves]
+
+        def quantize(values, width, tag):
+            codes = keep.tile([P, width], U32, name=f"{tag}_codes", align_bytes=64)
+            scales = keep.tile([P, width], U8, name=f"{tag}_scales", align_bytes=64)
+            nc.vector.quantize_mx(out=codes[:].bitcast(FP8X4), scales=scales[:], in_=values)
+            return codes, scales
+
+        def prepare_first(raw_halves, tag, copy):
+            grouped = keep.tile([P, PACK * H], BF16, name=f"{tag}_grouped", tag=f"{tag}_grouped", align_bytes=64)
+            view = grouped[:].rearrange("p (t m j) -> p m t j", t=PACK, j=PACK)
+            for u in range(2):
+                copy(view[:, u * 64 : (u + 1) * 64, :, :], raw_halves[u].rearrange("p j (m t) -> p m t j", t=PACK))
+            return [quantize(grouped[:, t * H : (t + 1) * H], P, f"{tag}{t}") for t in range(PACK)]
+
+        w1_q = prepare_first(w1_raw, "w1", nc.scalar.copy)
+
+        picked = []
+        for c in range(S // GATHER):
+            entries = offsets[:, c * GATHER // 16 : (c + 1) * GATHER // 16]
+            words = keep.tile([P, GATHER], U32, name=f"picked_words{c}", tag="w1_grouped" if c == 3 else f"picked_words{c}", align_bytes=64)
+            scales = keep.tile([P, GATHER], U8, name=f"picked_scales{c}", align_bytes=64)
+            nc.vector.tensor_copy(words[:], word_table[:].bitcast(U32).indirect(entries))
+            nc.vector.tensor_copy(scales[:], scale_table[:].indirect(entries))
+            picked.append((words, scales))
+
+        second_grouped = keep.tile([P, 2, N, PACK], BF16, name="second_grouped", align_bytes=64)
+        nc.scalar.copy(second_grouped[:, 0, :, :], w2_raw.rearrange("p j n -> p n j"))
+        nc.scalar.mul(second_grouped[:, 1, :, :], r2_raw.rearrange("p j n -> p n j"), -1.0)
+
+        r1_q = prepare_first(r1_raw, "r1", nc.vector.tensor_copy)
+        second_codes, second_scales = quantize(second_grouped[:].rearrange("p w n j -> p (w n j)"), 2 * N, "second")
+
+        def hidden_pair(weights, c, tag, vector_banks):
+            words, word_scales = picked[c]
+            values = keep.tile([P, PAIR, PACK], BF16, name=f"{tag}_values{c}", align_bytes=64)
+            for b in range(PAIR // BANK):
+                cols = slice(b * BANK, (b + 1) * BANK)
+                acc = hidden_psum.tile([P, PACK, BANK], F32, name="acc")
+                for t in range(PACK):
+                    codes, scales = weights[t]
+                    nc.tensor.matmul_mx(out=acc[:, t, :], lhsT=codes[:].bitcast(FP8X4), lhsT_scale=scales[:],
+                                        rhs=words[:, cols].bitcast(FP8X4), rhs_scale=word_scales[:, cols], start=True, stop=True)
+                stepped = acc[:].rearrange("p t n -> p n t")
+                if 2 * c + b in vector_banks:
+                    nc.vector.tensor_scalar_max(values[:, cols, :], stepped, 0.0)
+                else:
+                    nc.scalar.activation(values[:, cols, :], stepped, ACT.Relu)
+            return quantize(values[:].rearrange("p n t -> p (n t)"), PAIR, f"{tag}{c}")
+
+        h_q = [hidden_pair(w1_q, c, "h", H_VECTOR_BANKS) for c in range(S // PAIR)]
+        for c in range(S // PAIR):
+            g_q = hidden_pair(r1_q, c, "g", G_VECTOR_BANKS)
+            diff = diff_psum.tile([P, PAIR], F32, name="diff")
+            for w, (codes, scales) in enumerate((h_q[c], g_q)):
+                rows = slice(w * N, (w + 1) * N)
+                nc.tensor.matmul_mx(out=diff[:], lhsT=second_codes[:, rows].bitcast(FP8X4), lhsT_scale=second_scales[:, rows],
+                                    rhs=codes[:].bitcast(FP8X4), rhs_scale=scales[:], start=(w == 0), stop=(w == 1))
+            result = keep.tile([P, PAIR], F32, name=f"result{c}")
+            nc.scalar.activation(result[:], diff[:], ACT.Square)
+            nc.sync.dma_start(out=out[:, c * PAIR : (c + 1) * PAIR], in_=result[:])

@@ -20,45 +20,51 @@ GATHER = 256
 BANK = 128
 PAIR = 256
 HALF = H // 2
+LEAD = 320
+SHARE = 80
+AHEAD = 512
 H_VECTOR_BANKS = ()
-G_VECTOR_BANKS = (1, 3, 5, 7)
+G_VECTOR_BANKS = (0, 1, 3, 5)
+STRETCHES = ((0, 256), (256, 256), (512, 256), (768, 128), (896, 128))
 
 
 def tile_picked_yrnd_sq_p_kernel(tc, x_words, x_scales, w1, r1, w2, r2, offs, out):
     nc = tc.nc
     with ExitStack() as ctx:
         keep = ctx.enter_context(tc.tile_pool(name="keep", bufs=1))
-        hidden_psum = ctx.enter_context(tc.psum_pool(name="hidden_psum", bufs=6))
-        diff_psum = ctx.enter_context(tc.psum_pool(name="diff_psum", bufs=2))
+        hidden_psum = ctx.enter_context(tc.psum_pool(name="hidden_psum", bufs=5))
+        diff_psum = ctx.enter_context(tc.psum_pool(name="diff_psum", bufs=3))
 
         offsets = keep.tile([P, S // 16], U16, name="offsets")
         nc.sync.dma_start(offsets[:], offs)
 
-        scale_table = keep.tile([P, T], U8, name="scale_table", align_bytes=64)
-        nc.vector.memset(scale_table[:].bitcast(I32), 0)
-        word_table = keep.tile([P, T], I32, name="word_table", align_bytes=64)
-        nc.sync.dma_start(out=word_table[:], in_=x_words[0].rearrange("p n t -> p (n t)").bitcast(I32))
-        for q in range(4):
-            nc.sync.dma_start(out=scale_table[32 * q : 32 * q + 4, :].bitcast(I32), in_=x_scales[0, 4 * q : 4 * q + 4, :].bitcast(I32))
-
-        warm = keep.tile([P, 1], F32, name="warm", tag="raw")
-        nc.gpsimd.memset(warm[:], 0.0)
-        warm_out = keep.tile([P, 1], F32, name="warm_out")
-        nc.scalar.activation(warm_out[:], warm[:], ACT.Relu)
-
-        raw = keep.tile([P, PACK * (2 * H + 2 * N)], F32, name="raw", tag="raw")
-
-        def load(w, cols, place):
+        def load(w, cols, stage, place):
             width = cols.stop - cols.start
-            rows = raw[:, PACK * place : PACK * (place + width)].rearrange("p (j c) -> p j c", j=PACK)
+            rows = stage[:, PACK * place : PACK * (place + width)].rearrange("p (j c) -> p j c", j=PACK)
             nc.sync.dma_start(out=rows, in_=w.rearrange("(p j) c -> p j c", j=PACK)[:, :, cols])
             return rows
 
-        halves = [slice(0, HALF), slice(HALF, H)]
-        w1_raw = [load(w1, cols, cols.start) for cols in halves]
-        w2_raw = load(w2, slice(0, N), H)
-        r2_raw = load(r2, slice(0, N), H + N)
-        r1_raw = [load(r1, cols, H + 2 * N + cols.start) for cols in halves]
+        early = keep.tile([P, PACK * LEAD], F32, name="early")
+        w1_lead = load(w1, slice(0, LEAD), early, 0)
+
+        scale_table = keep.tile([P, T], U8, name="scale_table", align_bytes=64)
+        nc.vector.memset(scale_table[:].bitcast(I32), 0)
+        for q in range(4):
+            nc.sync.dma_start(out=scale_table[32 * q : 32 * q + 4, :].bitcast(I32), in_=x_scales[0, 4 * q : 4 * q + 4, :].bitcast(I32))
+
+        warm = keep.tile([P, 1], F32, name="warm", tag="late")
+        nc.gpsimd.memset(warm[:], 0.0)
+        warm_out = keep.tile([P, 1], F32, name="warm_out", tag="word_table", align_bytes=64)
+        nc.scalar.activation(warm_out[:], warm[:], ACT.Relu)
+
+        word_table = keep.tile([P, T], I32, name="word_table", tag="word_table", align_bytes=64)
+        nc.sync.dma_start(out=word_table[:], in_=x_words[0].rearrange("p n t -> p (n t)").bitcast(I32))
+
+        late = keep.tile([P, PACK * (2 * H - LEAD + 2 * N)], F32, name="late", tag="late")
+        w1_rest = load(w1, slice(LEAD, H), late, 0)
+        r1_raw = [load(r1, cols, late, H - LEAD + 2 * N + cols.start) for cols in (slice(0, HALF), slice(HALF, H))]
+        w2_raw = load(w2, slice(0, N), late, H - LEAD)
+        r2_raw = load(r2, slice(0, N), late, H - LEAD + N)
 
         def quantize(values, width, tag):
             codes = keep.tile([P, width], U32, name=f"{tag}_codes", align_bytes=64)
@@ -66,56 +72,65 @@ def tile_picked_yrnd_sq_p_kernel(tc, x_words, x_scales, w1, r1, w2, r2, offs, ou
             nc.vector.quantize_mx(out=codes[:].bitcast(FP8X4), scales=scales[:], in_=values)
             return codes, scales
 
-        def prepare_first(raw_halves, tag, copy):
+        def prepare_first(tag, copies):
             grouped = keep.tile([P, PACK * H], BF16, name=f"{tag}_grouped", tag=f"{tag}_grouped", align_bytes=64)
             view = grouped[:].rearrange("p (t m j) -> p m t j", t=PACK, j=PACK)
-            for u in range(2):
-                copy(view[:, u * 64 : (u + 1) * 64, :, :], raw_halves[u].rearrange("p j (m t) -> p m t j", t=PACK))
+            for rows, first, copy in copies:
+                copy(view[:, first // PACK : (first + rows.shape[2]) // PACK, :, :], rows.rearrange("p j (m t) -> p m t j", t=PACK))
             return [quantize(grouped[:, t * H : (t + 1) * H], P, f"{tag}{t}") for t in range(PACK)]
 
-        w1_q = prepare_first(w1_raw, "w1", nc.scalar.copy)
+        def entries(first, width):
+            return offsets[:, first // 16 : (first + width) // 16]
 
-        picked = []
-        for c in range(S // GATHER):
-            entries = offsets[:, c * GATHER // 16 : (c + 1) * GATHER // 16]
-            words = keep.tile([P, GATHER], U32, name=f"picked_words{c}", tag="w1_grouped" if c == 3 else f"picked_words{c}", align_bytes=64)
-            scales = keep.tile([P, GATHER], U8, name=f"picked_scales{c}", align_bytes=64)
-            nc.vector.tensor_copy(words[:], word_table[:].bitcast(U32).indirect(entries))
-            nc.vector.tensor_copy(scales[:], scale_table[:].indirect(entries))
-            picked.append((words, scales))
+        picked_scales = keep.tile([P, S], U8, name="picked_scales", align_bytes=64)
+        for first in range(0, S, 1024):
+            nc.vector.tensor_copy(picked_scales[:, first : first + 1024], scale_table[:].indirect(entries(first, 1024)))
 
+        def pick_words(start, stop, tag):
+            words = keep.tile([P, stop - start], U32, name=f"picked_words{start}", tag=tag, align_bytes=64)
+            for first in range(start, stop, GATHER):
+                nc.vector.tensor_copy(words[:, first - start : first - start + GATHER], word_table[:].bitcast(U32).indirect(entries(first, GATHER)))
+            return words
+
+        words_ahead = pick_words(0, AHEAD, "words_ahead")
+        w1_q = prepare_first("w1", [(w1_lead, 0, nc.scalar.copy), (w1_rest[:, :, 0:SHARE], LEAD, nc.scalar.copy), (w1_rest[:, :, SHARE:], LEAD + SHARE, nc.vector.tensor_copy)])
+        words_behind = pick_words(AHEAD, S, "w1_grouped")
+
+        r1_q = prepare_first("r1", [(r1_raw[0], 0, nc.scalar.copy), (r1_raw[1], HALF, nc.vector.tensor_copy)])
         second_grouped = keep.tile([P, 2, N, PACK], BF16, name="second_grouped", align_bytes=64)
-        nc.scalar.copy(second_grouped[:, 0, :, :], w2_raw.rearrange("p j n -> p n j"))
-        nc.scalar.mul(second_grouped[:, 1, :, :], r2_raw.rearrange("p j n -> p n j"), -1.0)
+        nc.vector.tensor_copy(second_grouped[:, 0, :, :], w2_raw.rearrange("p j n -> p n j"))
+        nc.vector.tensor_scalar_mul(second_grouped[:, 1, :, :], r2_raw.rearrange("p j n -> p n j"), -1.0)
 
-        r1_q = prepare_first(r1_raw, "r1", nc.vector.tensor_copy)
         second_codes, second_scales = quantize(second_grouped[:].rearrange("p w n j -> p (w n j)"), 2 * N, "second")
 
-        def hidden_pair(weights, c, tag, vector_banks):
-            words, word_scales = picked[c]
-            values = keep.tile([P, PAIR, PACK], BF16, name=f"{tag}_values{c}", align_bytes=64)
-            for b in range(PAIR // BANK):
-                cols = slice(b * BANK, (b + 1) * BANK)
+        def hidden(weights, first, width, tag, vector_banks):
+            values = keep.tile([P, width, PACK], BF16, name=f"{tag}_values{first}", align_bytes=64)
+            for b in range(width // BANK):
+                cols = slice(first + b * BANK, first + (b + 1) * BANK)
+                words = words_ahead[:, cols] if cols.start < AHEAD else words_behind[:, cols.start - AHEAD : cols.stop - AHEAD]
                 acc = hidden_psum.tile([P, PACK, BANK], F32, name="acc")
                 for t in range(PACK):
                     codes, scales = weights[t]
                     nc.tensor.matmul_mx(out=acc[:, t, :], lhsT=codes[:].bitcast(FP8X4), lhsT_scale=scales[:],
-                                        rhs=words[:, cols].bitcast(FP8X4), rhs_scale=word_scales[:, cols], start=True, stop=True)
+                                        rhs=words.bitcast(FP8X4), rhs_scale=picked_scales[:, cols], start=True, stop=True)
                 stepped = acc[:].rearrange("p t n -> p n t")
-                if 2 * c + b in vector_banks:
-                    nc.vector.tensor_scalar_max(values[:, cols, :], stepped, 0.0)
+                target = values[:, b * BANK : (b + 1) * BANK, :]
+                if cols.start // BANK in vector_banks:
+                    nc.vector.tensor_scalar_max(target, stepped, 0.0)
                 else:
-                    nc.scalar.activation(values[:, cols, :], stepped, ACT.Relu)
-            return quantize(values[:].rearrange("p n t -> p (n t)"), PAIR, f"{tag}{c}")
+                    nc.scalar.activation(target, stepped, ACT.Relu)
+            return quantize(values[:].rearrange("p n t -> p (n t)"), width, f"{tag}{first}")
 
-        h_q = [hidden_pair(w1_q, c, "h", H_VECTOR_BANKS) for c in range(S // PAIR)]
-        for c in range(S // PAIR):
-            g_q = hidden_pair(r1_q, c, "g", G_VECTOR_BANKS)
-            diff = diff_psum.tile([P, PAIR], F32, name="diff")
-            for w, (codes, scales) in enumerate((h_q[c], g_q)):
+        h_q = [hidden(w1_q, c * PAIR, PAIR, "h", H_VECTOR_BANKS) for c in range(S // PAIR)]
+        for first, width in STRETCHES:
+            g_codes, g_scales = hidden(r1_q, first, width, "g", G_VECTOR_BANKS)
+            h_codes, h_scales = h_q[first // PAIR]
+            inside = slice(first % PAIR, first % PAIR + width)
+            diff = diff_psum.tile([P, width], F32, name="diff")
+            for w, (codes, scales) in enumerate(((h_codes[:, inside], h_scales[:, inside]), (g_codes[:], g_scales[:]))):
                 rows = slice(w * N, (w + 1) * N)
                 nc.tensor.matmul_mx(out=diff[:], lhsT=second_codes[:, rows].bitcast(FP8X4), lhsT_scale=second_scales[:, rows],
-                                    rhs=codes[:].bitcast(FP8X4), rhs_scale=scales[:], start=(w == 0), stop=(w == 1))
-            result = keep.tile([P, PAIR], F32, name=f"result{c}")
+                                    rhs=codes.bitcast(FP8X4), rhs_scale=scales, start=(w == 0), stop=(w == 1))
+            result = keep.tile([P, width], F32, name=f"result{first}")
             nc.scalar.activation(result[:], diff[:], ACT.Square)
-            nc.sync.dma_start(out=out[:, c * PAIR : (c + 1) * PAIR], in_=result[:])
+            nc.sync.dma_start(out=out[:, first : first + width], in_=result[:])

@@ -74,9 +74,9 @@ def tile_picked_yrnd_sq_p_kernel(tc, x_words, x_scales, w1, r1, w2, r2, offs, ou
 
         def prepare_first(tag, copies):
             grouped = keep.tile([P, PACK * H], BF16, name=f"{tag}_grouped", tag=f"{tag}_grouped", align_bytes=64)
-            view = grouped[:].rearrange("p (t m j) -> p m t j", t=PACK, j=PACK)
+            view = grouped[:].rearrange("p (t m j) -> p m j t", t=PACK, j=PACK)
             for rows, first, copy in copies:
-                copy(view[:, first // PACK : (first + rows.shape[2]) // PACK, :, :], rows.rearrange("p j (m t) -> p m t j", t=PACK))
+                copy(view[:, first // PACK : (first + rows.shape[2]) // PACK, :, :], rows.rearrange("p j (m t) -> p m j t", t=PACK))
             return [quantize(grouped[:, t * H : (t + 1) * H], P, f"{tag}{t}") for t in range(PACK)]
 
         def entries(first, width):
@@ -98,8 +98,8 @@ def tile_picked_yrnd_sq_p_kernel(tc, x_words, x_scales, w1, r1, w2, r2, offs, ou
 
         r1_q = prepare_first("r1", [(r1_raw[0], 0, nc.scalar.copy), (r1_raw[1], HALF, nc.vector.tensor_copy)])
         second_grouped = keep.tile([P, 2, N, PACK], BF16, name="second_grouped", align_bytes=64)
-        nc.vector.tensor_copy(second_grouped[:, 0, :, :], w2_raw.rearrange("p j n -> p n j"))
-        nc.vector.tensor_scalar_mul(second_grouped[:, 1, :, :], r2_raw.rearrange("p j n -> p n j"), -1.0)
+        nc.vector.tensor_copy(second_grouped[:, 0, :, :].rearrange("p (c i) j -> p c j i", i=PACK), w2_raw.rearrange("p j (c i) -> p c j i", i=PACK))
+        nc.vector.tensor_scalar_mul(second_grouped[:, 1, :, :].rearrange("p (c i) j -> p c j i", i=PACK), r2_raw.rearrange("p j (c i) -> p c j i", i=PACK), -1.0)
 
         second_codes, second_scales = quantize(second_grouped[:].rearrange("p w n j -> p (w n j)"), 2 * N, "second")
 

@@ -20,11 +20,12 @@ GATHER = 256
 BANK = 128
 PAIR = 256
 HALF = H // 2
-LEAD = 320
+H_LEAD = 3
+LEAD = 384
 SHARE = 80
 AHEAD = 512
-H_VECTOR_BANKS = ()
-G_VECTOR_BANKS = (0, 1, 3, 5)
+H_VECTOR_BANKS = (7,)
+G_VECTOR_BANKS = (1, 3, 5)
 STRETCHES = ((0, 256), (256, 256), (512, 256), (768, 128), (896, 128))
 
 
@@ -72,12 +73,13 @@ def tile_picked_yrnd_sq_p_kernel(tc, x_words, x_scales, w1, r1, w2, r2, offs, ou
             nc.vector.quantize_mx(out=codes[:].bitcast(FP8X4), scales=scales[:], in_=values)
             return codes, scales
 
-        def prepare_first(tag, copies):
+        def prepare_first(tag, copies, width):
             grouped = keep.tile([P, PACK * H], BF16, name=f"{tag}_grouped", tag=f"{tag}_grouped", align_bytes=64)
             view = grouped[:].rearrange("p (t m j) -> p m j t", t=PACK, j=PACK)
             for rows, first, copy in copies:
                 copy(view[:, first // PACK : (first + rows.shape[2]) // PACK, :, :], rows.rearrange("p j (m t) -> p m j t", t=PACK))
-            return [quantize(grouped[:, t * H : (t + 1) * H], P, f"{tag}{t}") for t in range(PACK)]
+            made = [quantize(grouped[:, PACK * c : PACK * (c + width)], width, f"{tag}{c}") for c in range(0, H, width)]
+            return [(made[c // width][0][:, c % width : c % width + P], made[c // width][1][:, c % width : c % width + P]) for c in range(0, H, P)]
 
         def entries(first, width):
             return offsets[:, first // 16 : (first + width) // 16]
@@ -93,10 +95,10 @@ def tile_picked_yrnd_sq_p_kernel(tc, x_words, x_scales, w1, r1, w2, r2, offs, ou
             return words
 
         words_ahead = pick_words(0, AHEAD, "words_ahead")
-        w1_q = prepare_first("w1", [(w1_lead, 0, nc.scalar.copy), (w1_rest[:, :, 0:SHARE], LEAD, nc.scalar.copy), (w1_rest[:, :, SHARE:], LEAD + SHARE, nc.vector.tensor_copy)])
+        w1_q = prepare_first("w1", [(w1_lead, 0, nc.scalar.copy), (w1_rest, LEAD, nc.scalar.copy)], P)
         words_behind = pick_words(AHEAD, S, "w1_grouped")
 
-        r1_q = prepare_first("r1", [(r1_raw[0], 0, nc.scalar.copy), (r1_raw[1], HALF, nc.vector.tensor_copy)])
+        r1_q = prepare_first("r1", [(r1_raw[0], 0, nc.scalar.copy), (r1_raw[1], HALF, nc.vector.tensor_copy)], 512)
         second_grouped = keep.tile([P, 2, N, PACK], BF16, name="second_grouped", align_bytes=64)
         nc.vector.tensor_copy(second_grouped[:, 0, :, :].rearrange("p (c i) j -> p c j i", i=PACK), w2_raw.rearrange("p j (c i) -> p c j i", i=PACK))
         nc.vector.tensor_scalar_mul(second_grouped[:, 1, :, :].rearrange("p (c i) j -> p c j i", i=PACK), r2_raw.rearrange("p j (c i) -> p c j i", i=PACK), -1.0)
@@ -111,7 +113,7 @@ def tile_picked_yrnd_sq_p_kernel(tc, x_words, x_scales, w1, r1, w2, r2, offs, ou
                 acc = hidden_psum.tile([P, PACK, BANK], F32, name="acc")
                 for t in range(PACK):
                     codes, scales = weights[t]
-                    nc.tensor.matmul_mx(out=acc[:, t, :], lhsT=codes[:].bitcast(FP8X4), lhsT_scale=scales[:],
+                    nc.tensor.matmul_mx(out=acc[:, t, :], lhsT=codes.bitcast(FP8X4), lhsT_scale=scales,
                                         rhs=words.bitcast(FP8X4), rhs_scale=picked_scales[:, cols], start=True, stop=True)
                 stepped = acc[:].rearrange("p t n -> p n t")
                 target = values[:, b * BANK : (b + 1) * BANK, :]
@@ -121,8 +123,10 @@ def tile_picked_yrnd_sq_p_kernel(tc, x_words, x_scales, w1, r1, w2, r2, offs, ou
                     nc.scalar.activation(target, stepped, ACT.Relu)
             return quantize(values[:].rearrange("p n t -> p (n t)"), width, f"{tag}{first}")
 
-        h_q = [hidden(w1_q, c * PAIR, PAIR, "h", H_VECTOR_BANKS) for c in range(S // PAIR)]
+        h_q = [hidden(w1_q, c * PAIR, PAIR, "h", H_VECTOR_BANKS) for c in range(H_LEAD)]
         for first, width in STRETCHES:
+            if first > 0 and len(h_q) < S // PAIR:
+                h_q.append(hidden(w1_q, len(h_q) * PAIR, PAIR, "h", H_VECTOR_BANKS))
             g_codes, g_scales = hidden(r1_q, first, width, "g", G_VECTOR_BANKS)
             h_codes, h_scales = h_q[first // PAIR]
             inside = slice(first % PAIR, first % PAIR + width)

@@ -20,12 +20,11 @@ GATHER = 256
 BANK = 128
 PAIR = 256
 HALF = H // 2
-H_LEAD = 3
+H_LEAD = 4
 LEAD = 384
-SHARE = 80
 AHEAD = 512
-H_VECTOR_BANKS = (7,)
-G_VECTOR_BANKS = (1, 3, 5)
+H_VECTOR_BANKS = ()
+G_VECTOR_BANKS = (0, 1, 4, 6)
 STRETCHES = ((0, 256), (256, 256), (512, 256), (768, 128), (896, 128))
 
 
@@ -33,8 +32,7 @@ def tile_picked_yrnd_sq_p_kernel(tc, x_words, x_scales, w1, r1, w2, r2, offs, ou
     nc = tc.nc
     with ExitStack() as ctx:
         keep = ctx.enter_context(tc.tile_pool(name="keep", bufs=1))
-        hidden_psum = ctx.enter_context(tc.psum_pool(name="hidden_psum", bufs=5))
-        diff_psum = ctx.enter_context(tc.psum_pool(name="diff_psum", bufs=3))
+        psum = ctx.enter_context(tc.psum_pool(name="psum", bufs=1))
 
         offsets = keep.tile([P, S // 16], U16, name="offsets")
         nc.sync.dma_start(offsets[:], offs)
@@ -110,7 +108,7 @@ def tile_picked_yrnd_sq_p_kernel(tc, x_words, x_scales, w1, r1, w2, r2, offs, ou
             for b in range(width // BANK):
                 cols = slice(first + b * BANK, first + (b + 1) * BANK)
                 words = words_ahead[:, cols] if cols.start < AHEAD else words_behind[:, cols.start - AHEAD : cols.stop - AHEAD]
-                acc = hidden_psum.tile([P, PACK, BANK], F32, name="acc")
+                acc = psum.tile([P, PACK, BANK], F32, name=f"{tag}_acc{cols.start}", tag=f"bank{cols.start // BANK}")
                 for t in range(PACK):
                     codes, scales = weights[t]
                     nc.tensor.matmul_mx(out=acc[:, t, :], lhsT=codes.bitcast(FP8X4), lhsT_scale=scales,
@@ -130,7 +128,7 @@ def tile_picked_yrnd_sq_p_kernel(tc, x_words, x_scales, w1, r1, w2, r2, offs, ou
             g_codes, g_scales = hidden(r1_q, first, width, "g", G_VECTOR_BANKS)
             h_codes, h_scales = h_q[first // PAIR]
             inside = slice(first % PAIR, first % PAIR + width)
-            diff = diff_psum.tile([P, width], F32, name="diff")
+            diff = psum.tile([P, width], F32, name=f"diff{first}", tag=f"bank{first // BANK}")
             for w, (codes, scales) in enumerate(((h_codes[:, inside], h_scales[:, inside]), (g_codes[:], g_scales[:]))):
                 rows = slice(w * N, (w + 1) * N)
                 nc.tensor.matmul_mx(out=diff[:], lhsT=second_codes[:, rows].bitcast(FP8X4), lhsT_scale=second_scales[:, rows],

@@ -25,7 +25,7 @@ LEAD = 384
 AHEAD = 512
 H_VECTOR_BANKS = ()
 G_VECTOR_BANKS = (0, 1, 4, 6)
-STRETCHES = ((0, 256), (256, 256), (512, 256), (768, 128), (896, 128))
+STRETCHES = ((0, 256), (256, 256), (512, 256), (768, 256))
 
 
 def tile_picked_yrnd_sq_p_kernel(tc, x_words, x_scales, w1, r1, w2, r2, offs, out):
@@ -93,7 +93,7 @@ def tile_picked_yrnd_sq_p_kernel(tc, x_words, x_scales, w1, r1, w2, r2, offs, ou
             return words
 
         words_ahead = pick_words(0, AHEAD, "words_ahead")
-        w1_q = prepare_first("w1", [(w1_lead, 0, nc.scalar.copy), (w1_rest, LEAD, nc.scalar.copy)], P)
+        w1_q = prepare_first("w1", [(w1_lead, 0, nc.scalar.copy), (w1_rest, LEAD, nc.scalar.copy)], HALF)
         words_behind = pick_words(AHEAD, S, "w1_grouped")
 
         r1_q = prepare_first("r1", [(r1_raw[0], 0, nc.scalar.copy), (r1_raw[1], HALF, nc.vector.tensor_copy)], 512)

@@ -51,11 +51,6 @@ def tile_picked_yrnd_sq_p_kernel(tc, x_words, x_scales, w1, r1, w2, r2, offs, ou
         for q in range(4):
             nc.sync.dma_start(out=scale_table[32 * q : 32 * q + 4, :].bitcast(I32), in_=x_scales[0, 4 * q : 4 * q + 4, :].bitcast(I32))
 
-        warm = keep.tile([P, 1], F32, name="warm", tag="late")
-        nc.gpsimd.memset(warm[:], 0.0)
-        warm_out = keep.tile([P, 1], F32, name="warm_out", tag="word_table", align_bytes=64)
-        nc.scalar.activation(warm_out[:], warm[:], ACT.Relu)
-
         word_table = keep.tile([P, T], I32, name="word_table", tag="word_table", align_bytes=64)
         nc.sync.dma_start(out=word_table[:], in_=x_words[0].rearrange("p n t -> p (n t)").bitcast(I32))
 

@@ -16,16 +16,13 @@ ACT = mybir.ActivationFunctionType
 
 P = 128
 PACK = 4
-GATHER = 256
 BANK = 128
-PAIR = 256
-HALF = H // 2
-H_LEAD = 4
-LEAD = 384
-AHEAD = 512
+LEAD = 256
+GATHERS = (256, 256, 512)
+H_QUANTIZE = 512
+STRETCH = 256
 H_VECTOR_BANKS = ()
-G_VECTOR_BANKS = (0, 1, 4, 6)
-STRETCHES = ((0, 256), (256, 256), (512, 256), (768, 256))
+G_VECTOR_BANKS = (0, 2, 4, 6)
 
 
 def tile_picked_yrnd_sq_p_kernel(tc, x_words, x_scales, w1, r1, w2, r2, offs, out):
@@ -34,31 +31,28 @@ def tile_picked_yrnd_sq_p_kernel(tc, x_words, x_scales, w1, r1, w2, r2, offs, ou
         keep = ctx.enter_context(tc.tile_pool(name="keep", bufs=1))
         psum = ctx.enter_context(tc.psum_pool(name="psum", bufs=1))
 
-        offsets = keep.tile([P, S // 16], U16, name="offsets")
-        nc.sync.dma_start(offsets[:], offs)
-
-        def load(w, cols, stage, place):
-            width = cols.stop - cols.start
-            rows = stage[:, PACK * place : PACK * (place + width)].rearrange("p (j c) -> p j c", j=PACK)
-            nc.sync.dma_start(out=rows, in_=w.rearrange("(p j) c -> p j c", j=PACK)[:, :, cols])
+        def load(w, cols, name):
+            rows = keep.tile([P, PACK, cols.stop - cols.start], F32, name=name, tag=name, align_bytes=64)
+            nc.sync.dma_start(out=rows[:], in_=w.rearrange("(p j) c -> p j c", j=PACK)[:, :, cols])
             return rows
 
-        early = keep.tile([P, PACK * LEAD], F32, name="early")
-        w1_lead = load(w1, slice(0, LEAD), early, 0)
+        w1_lead = load(w1, slice(0, LEAD), "w1_lead")
+
+        offsets = keep.tile([P, S // 16], U16, name="offsets")
+        nc.sync.dma_start(offsets[:], offs)
 
         scale_table = keep.tile([P, T], U8, name="scale_table", align_bytes=64)
         nc.vector.memset(scale_table[:].bitcast(I32), 0)
         for q in range(4):
             nc.sync.dma_start(out=scale_table[32 * q : 32 * q + 4, :].bitcast(I32), in_=x_scales[0, 4 * q : 4 * q + 4, :].bitcast(I32))
 
-        word_table = keep.tile([P, T], I32, name="word_table", tag="word_table", align_bytes=64)
+        w1_rest = load(w1, slice(LEAD, H), "w1_rest")
+        word_table = keep.tile([P, T], I32, name="word_table", align_bytes=64)
         nc.sync.dma_start(out=word_table[:], in_=x_words[0].rearrange("p n t -> p (n t)").bitcast(I32))
-
-        late = keep.tile([P, PACK * (2 * H - LEAD + 2 * N)], F32, name="late", tag="late")
-        w1_rest = load(w1, slice(LEAD, H), late, 0)
-        r1_raw = [load(r1, cols, late, H - LEAD + 2 * N + cols.start) for cols in (slice(0, HALF), slice(HALF, H))]
-        w2_raw = load(w2, slice(0, N), late, H - LEAD)
-        r2_raw = load(r2, slice(0, N), late, H - LEAD + N)
+        r1_lead = load(r1, slice(0, LEAD), "r1_lead")
+        r1_rest = load(r1, slice(LEAD, H), "r1_rest")
+        w2_raw = load(w2, slice(0, N), "w2_raw")
+        r2_raw = load(r2, slice(0, N), "r2_raw")
 
         def quantize(values, width, tag):
             codes = keep.tile([P, width], U32, name=f"{tag}_codes", align_bytes=64)
@@ -66,68 +60,67 @@ def tile_picked_yrnd_sq_p_kernel(tc, x_words, x_scales, w1, r1, w2, r2, offs, ou
             nc.vector.quantize_mx(out=codes[:].bitcast(FP8X4), scales=scales[:], in_=values)
             return codes, scales
 
-        def prepare_first(tag, copies, width):
-            grouped = keep.tile([P, PACK * H], BF16, name=f"{tag}_grouped", tag=f"{tag}_grouped", align_bytes=64)
+        def prepare_first(tag, copies):
+            grouped = keep.tile([P, PACK * H], BF16, name=f"{tag}_grouped", align_bytes=64)
             view = grouped[:].rearrange("p (t m j) -> p m j t", t=PACK, j=PACK)
             for rows, first, copy in copies:
                 copy(view[:, first // PACK : (first + rows.shape[2]) // PACK, :, :], rows.rearrange("p j (m t) -> p m j t", t=PACK))
-            made = [quantize(grouped[:, PACK * c : PACK * (c + width)], width, f"{tag}{c}") for c in range(0, H, width)]
-            return [(made[c // width][0][:, c % width : c % width + P], made[c // width][1][:, c % width : c % width + P]) for c in range(0, H, P)]
+            return quantize(grouped[:], H, tag)
 
         def entries(first, width):
             return offsets[:, first // 16 : (first + width) // 16]
 
         picked_scales = keep.tile([P, S], U8, name="picked_scales", align_bytes=64)
-        for first in range(0, S, 1024):
-            nc.vector.tensor_copy(picked_scales[:, first : first + 1024], scale_table[:].indirect(entries(first, 1024)))
+        nc.vector.tensor_copy(picked_scales[:], scale_table[:].indirect(entries(0, S)))
 
-        def pick_words(start, stop, tag):
-            words = keep.tile([P, stop - start], U32, name=f"picked_words{start}", tag=tag, align_bytes=64)
-            for first in range(start, stop, GATHER):
-                nc.vector.tensor_copy(words[:, first - start : first - start + GATHER], word_table[:].bitcast(U32).indirect(entries(first, GATHER)))
-            return words
+        w1_q = prepare_first("w1", [(w1_lead[:], 0, nc.scalar.copy), (w1_rest[:], LEAD, nc.scalar.copy)])
 
-        words_ahead = pick_words(0, AHEAD, "words_ahead")
-        w1_q = prepare_first("w1", [(w1_lead, 0, nc.scalar.copy), (w1_rest, LEAD, nc.scalar.copy)], HALF)
-        words_behind = pick_words(AHEAD, S, "w1_grouped")
+        picked_words = keep.tile([P, S], U32, name="picked_words", tag="w1_rest", align_bytes=64)
+        first = 0
+        for width in GATHERS:
+            nc.vector.tensor_copy(picked_words[:, first : first + width], word_table[:].bitcast(U32).indirect(entries(first, width)))
+            first = first + width
 
-        r1_q = prepare_first("r1", [(r1_raw[0], 0, nc.scalar.copy), (r1_raw[1], HALF, nc.vector.tensor_copy)], 512)
+        r1_q = prepare_first("r1", [(r1_lead[:], 0, nc.scalar.copy), (r1_rest[:], LEAD, nc.vector.tensor_copy)])
+
+        def hidden(weights, tag, slot, vector_banks):
+            codes, scales = weights
+            values = keep.tile([P, S, PACK], BF16, name=f"{tag}_values", tag=slot, align_bytes=64)
+            for b in range(S // BANK):
+                cols = slice(b * BANK, (b + 1) * BANK)
+                acc = psum.tile([P, PACK, BANK], F32, name=f"{tag}_acc{b}", tag=f"bank{b}")
+                for t in range(PACK):
+                    group = slice(t * P, (t + 1) * P)
+                    nc.tensor.matmul_mx(out=acc[:, t, :], lhsT=codes[:, group].bitcast(FP8X4), lhsT_scale=scales[:, group],
+                                        rhs=picked_words[:, cols].bitcast(FP8X4), rhs_scale=picked_scales[:, cols], start=True, stop=True)
+                stepped = acc[:].rearrange("p t n -> p n t")
+                if b in vector_banks:
+                    nc.vector.tensor_scalar_max(values[:, cols, :], stepped, 0.0)
+                else:
+                    nc.scalar.activation(values[:, cols, :], stepped, ACT.Relu)
+            return values[:].rearrange("p n t -> p (n t)")
+
+        h_values = hidden(w1_q, "h", "r1_lead", H_VECTOR_BANKS)
+        h_codes = keep.tile([P, S], U32, name="h_codes", tag="r1_rest", align_bytes=64)
+        h_scales = keep.tile([P, S], U8, name="h_scales", align_bytes=64)
+        for first in range(0, S, H_QUANTIZE):
+            cols = slice(first, first + H_QUANTIZE)
+            nc.vector.quantize_mx(out=h_codes[:, cols].bitcast(FP8X4), scales=h_scales[:, cols], in_=h_values[:, PACK * cols.start : PACK * cols.stop])
+
         second_grouped = keep.tile([P, 2, N, PACK], BF16, name="second_grouped", align_bytes=64)
-        nc.vector.tensor_copy(second_grouped[:, 0, :, :].rearrange("p (c i) j -> p c j i", i=PACK), w2_raw.rearrange("p j (c i) -> p c j i", i=PACK))
-        nc.vector.tensor_scalar_mul(second_grouped[:, 1, :, :].rearrange("p (c i) j -> p c j i", i=PACK), r2_raw.rearrange("p j (c i) -> p c j i", i=PACK), -1.0)
-
+        nc.vector.tensor_copy(second_grouped[:, 0, :, :].rearrange("p (c i) j -> p c j i", i=PACK), w2_raw[:].rearrange("p j (c i) -> p c j i", i=PACK))
+        nc.vector.tensor_scalar_mul(second_grouped[:, 1, :, :].rearrange("p (c i) j -> p c j i", i=PACK), r2_raw[:].rearrange("p j (c i) -> p c j i", i=PACK), -1.0)
         second_codes, second_scales = quantize(second_grouped[:].rearrange("p w n j -> p (w n j)"), 2 * N, "second")
 
-        def hidden(weights, first, width, tag, vector_banks):
-            values = keep.tile([P, width, PACK], BF16, name=f"{tag}_values{first}", align_bytes=64)
-            for b in range(width // BANK):
-                cols = slice(first + b * BANK, first + (b + 1) * BANK)
-                words = words_ahead[:, cols] if cols.start < AHEAD else words_behind[:, cols.start - AHEAD : cols.stop - AHEAD]
-                acc = psum.tile([P, PACK, BANK], F32, name=f"{tag}_acc{cols.start}", tag=f"bank{cols.start // BANK}")
-                for t in range(PACK):
-                    codes, scales = weights[t]
-                    nc.tensor.matmul_mx(out=acc[:, t, :], lhsT=codes.bitcast(FP8X4), lhsT_scale=scales,
-                                        rhs=words.bitcast(FP8X4), rhs_scale=picked_scales[:, cols], start=True, stop=True)
-                stepped = acc[:].rearrange("p t n -> p n t")
-                target = values[:, b * BANK : (b + 1) * BANK, :]
-                if cols.start // BANK in vector_banks:
-                    nc.vector.tensor_scalar_max(target, stepped, 0.0)
-                else:
-                    nc.scalar.activation(target, stepped, ACT.Relu)
-            return quantize(values[:].rearrange("p n t -> p (n t)"), width, f"{tag}{first}")
-
-        h_q = [hidden(w1_q, c * PAIR, PAIR, "h", H_VECTOR_BANKS) for c in range(H_LEAD)]
-        for first, width in STRETCHES:
-            if first > 0 and len(h_q) < S // PAIR:
-                h_q.append(hidden(w1_q, len(h_q) * PAIR, PAIR, "h", H_VECTOR_BANKS))
-            g_codes, g_scales = hidden(r1_q, first, width, "g", G_VECTOR_BANKS)
-            h_codes, h_scales = h_q[first // PAIR]
-            inside = slice(first % PAIR, first % PAIR + width)
-            diff = psum.tile([P, width], F32, name=f"diff{first}", tag=f"bank{first // BANK}")
+        g_values = hidden(r1_q, "g", "g_values", G_VECTOR_BANKS)
+        for first in range(0, S, STRETCH):
+            inside = slice(first, first + STRETCH)
+            g_codes, g_scales = quantize(g_values[:, PACK * first : PACK * (first + STRETCH)], STRETCH, f"g{first}")
+            diff = psum.tile([P, STRETCH], F32, name=f"diff{first}", tag=f"bank{first // BANK}")
             for w, (codes, scales) in enumerate(((h_codes[:, inside], h_scales[:, inside]), (g_codes[:], g_scales[:]))):
                 rows = slice(w * N, (w + 1) * N)
                 nc.tensor.matmul_mx(out=diff[:], lhsT=second_codes[:, rows].bitcast(FP8X4), lhsT_scale=second_scales[:, rows],
                                     rhs=codes.bitcast(FP8X4), rhs_scale=scales, start=(w == 0), stop=(w == 1))
-            result = keep.tile([P, width], F32, name=f"result{first}")
+            result = keep.tile([P, STRETCH], F32, name=f"result{first}")
             nc.scalar.activation(result[:], diff[:], ACT.Square)
-            nc.sync.dma_start(out=out[:, first : first + width], in_=result[:])
+            nc.sync.dma_start(out=out[:, first : first + STRETCH], in_=result[:])

@@ -19,10 +19,10 @@ PACK = 4
 BANK = 128
 LEAD = 256
 GATHERS = (256, 256, 512)
-H_QUANTIZE = 512
-STRETCH = 256
-H_VECTOR_BANKS = ()
-G_VECTOR_BANKS = (0, 2, 4, 6)
+STRETCHES = ((0, 256), (256, 256), (512, 256), (768, 128), (896, 128))
+STORE_ENDS = (256, 512, 896, 1024)
+H_VECTOR_BANKS = {6: 64}
+G_VECTOR_BANKS = {0: 0, 2: 0, 4: 0}
 
 
 def tile_picked_yrnd_sq_p_kernel(tc, x_words, x_scales, w1, r1, w2, r2, offs, out):
@@ -49,10 +49,10 @@ def tile_picked_yrnd_sq_p_kernel(tc, x_words, x_scales, w1, r1, w2, r2, offs, ou
         w1_rest = load(w1, slice(LEAD, H), "w1_rest")
         word_table = keep.tile([P, T], I32, name="word_table", align_bytes=64)
         nc.sync.dma_start(out=word_table[:], in_=x_words[0].rearrange("p n t -> p (n t)").bitcast(I32))
-        r1_lead = load(r1, slice(0, LEAD), "r1_lead")
-        r1_rest = load(r1, slice(LEAD, H), "r1_rest")
         w2_raw = load(w2, slice(0, N), "w2_raw")
         r2_raw = load(r2, slice(0, N), "r2_raw")
+        r1_lead = load(r1, slice(0, LEAD), "r1_lead")
+        r1_rest = load(r1, slice(LEAD, H), "r1_rest")
 
         def quantize(values, width, tag):
             codes = keep.tile([P, width], U32, name=f"{tag}_codes", align_bytes=64)
@@ -61,7 +61,7 @@ def tile_picked_yrnd_sq_p_kernel(tc, x_words, x_scales, w1, r1, w2, r2, offs, ou
             return codes, scales
 
         def prepare_first(tag, copies):
-            grouped = keep.tile([P, PACK * H], BF16, name=f"{tag}_grouped", align_bytes=64)
+            grouped = keep.tile([P, PACK * H], BF16, name=f"{tag}_grouped", tag=f"{tag}_grouped", align_bytes=64)
             view = grouped[:].rearrange("p (t m j) -> p m j t", t=PACK, j=PACK)
             for rows, first, copy in copies:
                 copy(view[:, first // PACK : (first + rows.shape[2]) // PACK, :, :], rows.rearrange("p j (m t) -> p m j t", t=PACK))
@@ -81,12 +81,17 @@ def tile_picked_yrnd_sq_p_kernel(tc, x_words, x_scales, w1, r1, w2, r2, offs, ou
             nc.vector.tensor_copy(picked_words[:, first : first + width], word_table[:].bitcast(U32).indirect(entries(first, width)))
             first = first + width
 
-        r1_q = prepare_first("r1", [(r1_lead[:], 0, nc.scalar.copy), (r1_rest[:], LEAD, nc.vector.tensor_copy)])
+        second_grouped = keep.tile([P, 2, N, PACK], BF16, name="second_grouped", align_bytes=64)
+        nc.scalar.copy(second_grouped[:, 0, :, :].rearrange("p (c i) j -> p c j i", i=PACK), w2_raw[:].rearrange("p j (c i) -> p c j i", i=PACK))
+        nc.scalar.activation(second_grouped[:, 1, :, :].rearrange("p (c i) j -> p c j i", i=PACK), r2_raw[:].rearrange("p j (c i) -> p c j i", i=PACK), ACT.Copy, scale=-1.0)
 
-        def hidden(weights, tag, slot, vector_banks):
+        r1_q = prepare_first("r1", [(r1_lead[:], 0, nc.vector.tensor_copy), (r1_rest[:], LEAD, nc.vector.tensor_copy)])
+        second_codes, second_scales = quantize(second_grouped[:].rearrange("p w n j -> p (w n j)"), 2 * N, "second")
+
+        def hidden(weights, first, width, tag, slot, vector_banks):
             codes, scales = weights
-            values = keep.tile([P, S, PACK], BF16, name=f"{tag}_values", tag=slot, align_bytes=64)
-            for b in range(S // BANK):
+            values = keep.tile([P, width, PACK], BF16, name=f"{tag}_values{first}", tag=slot, align_bytes=64)
+            for b in range(first // BANK, (first + width) // BANK):
                 cols = slice(b * BANK, (b + 1) * BANK)
                 acc = psum.tile([P, PACK, BANK], F32, name=f"{tag}_acc{b}", tag=f"bank{b}")
                 for t in range(PACK):
@@ -94,33 +99,38 @@ def tile_picked_yrnd_sq_p_kernel(tc, x_words, x_scales, w1, r1, w2, r2, offs, ou
                     nc.tensor.matmul_mx(out=acc[:, t, :], lhsT=codes[:, group].bitcast(FP8X4), lhsT_scale=scales[:, group],
                                         rhs=picked_words[:, cols].bitcast(FP8X4), rhs_scale=picked_scales[:, cols], start=True, stop=True)
                 stepped = acc[:].rearrange("p t n -> p n t")
-                if b in vector_banks:
-                    nc.vector.tensor_scalar_max(values[:, cols, :], stepped, 0.0)
-                else:
-                    nc.scalar.activation(values[:, cols, :], stepped, ACT.Relu)
+                target = values[:, cols.start - first : cols.stop - first, :]
+                split = vector_banks.get(b, BANK)
+                if split > 0:
+                    nc.scalar.activation(target[:, :split, :], stepped[:, :split, :], ACT.Relu)
+                if split < BANK:
+                    nc.vector.tensor_scalar_max(target[:, split:, :], stepped[:, split:, :], 0.0)
             return values[:].rearrange("p n t -> p (n t)")
 
-        h_values = hidden(w1_q, "h", "r1_lead", H_VECTOR_BANKS)
         h_codes = keep.tile([P, S], U32, name="h_codes", tag="r1_rest", align_bytes=64)
         h_scales = keep.tile([P, S], U8, name="h_scales", align_bytes=64)
-        for first in range(0, S, H_QUANTIZE):
-            cols = slice(first, first + H_QUANTIZE)
-            nc.vector.quantize_mx(out=h_codes[:, cols].bitcast(FP8X4), scales=h_scales[:, cols], in_=h_values[:, PACK * cols.start : PACK * cols.stop])
+        for first, width, slot in ((0, 512, "r2_raw"), (512, 256, "h_middle"), (768, 256, "r1_grouped")):
+            h_values = hidden(w1_q, first, width, "h", slot, H_VECTOR_BANKS)
+            cols = slice(first, first + width)
+            nc.vector.quantize_mx(out=h_codes[:, cols].bitcast(FP8X4), scales=h_scales[:, cols], in_=h_values)
 
-        second_grouped = keep.tile([P, 2, N, PACK], BF16, name="second_grouped", align_bytes=64)
-        nc.vector.tensor_copy(second_grouped[:, 0, :, :].rearrange("p (c i) j -> p c j i", i=PACK), w2_raw[:].rearrange("p j (c i) -> p c j i", i=PACK))
-        nc.vector.tensor_scalar_mul(second_grouped[:, 1, :, :].rearrange("p (c i) j -> p c j i", i=PACK), r2_raw[:].rearrange("p j (c i) -> p c j i", i=PACK), -1.0)
-        second_codes, second_scales = quantize(second_grouped[:].rearrange("p w n j -> p (w n j)"), 2 * N, "second")
+        g_q = []
+        for first in (0, S // 2):
+            g_values = hidden(r1_q, first, S // 2, "g", f"g_values{first}", G_VECTOR_BANKS)
+            for start, width in STRETCHES:
+                if first <= start < first + S // 2:
+                    g_q.append(quantize(g_values[:, PACK * (start - first) : PACK * (start - first + width)], width, f"g{start}"))
 
-        g_values = hidden(r1_q, "g", "g_values", G_VECTOR_BANKS)
-        for first in range(0, S, STRETCH):
-            inside = slice(first, first + STRETCH)
-            g_codes, g_scales = quantize(g_values[:, PACK * first : PACK * (first + STRETCH)], STRETCH, f"g{first}")
-            diff = psum.tile([P, STRETCH], F32, name=f"diff{first}", tag=f"bank{first // BANK}")
+        result = keep.tile([P, S], F32, name="result")
+        stored = 0
+        for (first, width), (g_codes, g_scales) in zip(STRETCHES, g_q):
+            inside = slice(first, first + width)
+            diff = psum.tile([P, width], F32, name=f"diff{first}", tag=f"bank{first // BANK}")
             for w, (codes, scales) in enumerate(((h_codes[:, inside], h_scales[:, inside]), (g_codes[:], g_scales[:]))):
                 rows = slice(w * N, (w + 1) * N)
                 nc.tensor.matmul_mx(out=diff[:], lhsT=second_codes[:, rows].bitcast(FP8X4), lhsT_scale=second_scales[:, rows],
                                     rhs=codes.bitcast(FP8X4), rhs_scale=scales, start=(w == 0), stop=(w == 1))
-            result = keep.tile([P, STRETCH], F32, name=f"result{first}")
-            nc.scalar.activation(result[:], diff[:], ACT.Square)
-            nc.sync.dma_start(out=out[:, first : first + STRETCH], in_=result[:])
+            nc.scalar.activation(result[:, inside], diff[:], ACT.Square)
+            if inside.stop in STORE_ENDS:
+                nc.sync.dma_start(out=out[:, stored : inside.stop], in_=result[:, stored : inside.stop])
+                stored = inside.stop

@@ -21,8 +21,8 @@ LEAD = 256
 GATHERS = (256, 256, 512)
 STRETCHES = ((0, 256), (256, 256), (512, 256), (768, 128), (896, 128))
 STORE_ENDS = (256, 512, 896, 1024)
-H_VECTOR_BANKS = {6: 64}
-G_VECTOR_BANKS = {0: 0, 2: 0, 4: 0}
+H_VECTOR_BANKS = {7: 64}
+G_VECTOR_BANKS = {0: 0, 2: 0, 3: 0}
 
 
 def tile_picked_yrnd_sq_p_kernel(tc, x_words, x_scales, w1, r1, w2, r2, offs, out):
@@ -85,7 +85,17 @@ def tile_picked_yrnd_sq_p_kernel(tc, x_words, x_scales, w1, r1, w2, r2, offs, ou
         nc.scalar.copy(second_grouped[:, 0, :, :].rearrange("p (c i) j -> p c j i", i=PACK), w2_raw[:].rearrange("p j (c i) -> p c j i", i=PACK))
         nc.scalar.activation(second_grouped[:, 1, :, :].rearrange("p (c i) j -> p c j i", i=PACK), r2_raw[:].rearrange("p j (c i) -> p c j i", i=PACK), ACT.Copy, scale=-1.0)
 
-        r1_q = prepare_first("r1", [(r1_lead[:], 0, nc.vector.tensor_copy), (r1_rest[:], LEAD, nc.vector.tensor_copy)])
+        r1_grouped = keep.tile([P, PACK * H], BF16, name="r1_grouped", tag="r1_grouped", align_bytes=64)
+        r1_view = r1_grouped[:].rearrange("p (t m j) -> p m j t", t=PACK, j=PACK)
+        nc.vector.tensor_copy(r1_view[:, : LEAD // PACK, :, :], r1_lead[:].rearrange("p j (m t) -> p m j t", t=PACK))
+        for t in (0, 2):
+            nc.vector.tensor_copy(r1_view[:, LEAD // PACK :, :, t : t + 2], r1_rest[:].rearrange("p j (m t) -> p m j t", t=PACK)[:, :, :, t : t + 2])
+        r1_codes = keep.tile([P, H], U32, name="r1_codes", align_bytes=64)
+        r1_scales = keep.tile([P, H], U8, name="r1_scales", align_bytes=64)
+        for t in (0, 2):
+            cols = slice(t * P, (t + 2) * P)
+            nc.vector.quantize_mx(out=r1_codes[:, cols].bitcast(FP8X4), scales=r1_scales[:, cols], in_=r1_grouped[:, PACK * cols.start : PACK * cols.stop])
+        r1_q = (r1_codes, r1_scales)
         second_codes, second_scales = quantize(second_grouped[:].rearrange("p w n j -> p (w n j)"), 2 * N, "second")
 
         def hidden(weights, first, width, tag, slot, vector_banks):
@@ -101,10 +111,10 @@ def tile_picked_yrnd_sq_p_kernel(tc, x_words, x_scales, w1, r1, w2, r2, offs, ou
                 stepped = acc[:].rearrange("p t n -> p n t")
                 target = values[:, cols.start - first : cols.stop - first, :]
                 split = vector_banks.get(b, BANK)
-                if split > 0:
-                    nc.scalar.activation(target[:, :split, :], stepped[:, :split, :], ACT.Relu)
                 if split < BANK:
                     nc.vector.tensor_scalar_max(target[:, split:, :], stepped[:, split:, :], 0.0)
+                if split > 0:
+                    nc.scalar.activation(target[:, :split, :], stepped[:, :split, :], ACT.Relu)
             return values[:].rearrange("p n t -> p (n t)")
 
         h_codes = keep.tile([P, S], U32, name="h_codes", tag="r1_rest", align_bytes=64)

@@ -43,8 +43,8 @@ def tile_picked_yrnd_sq_p_kernel(tc, x_words, x_scales, w1, r1, w2, r2, offs, ou
 
         scale_table = keep.tile([P, T], U8, name="scale_table", align_bytes=64)
         nc.vector.memset(scale_table[:].bitcast(I32), 0)
-        for q in range(4):
-            nc.sync.dma_start(out=scale_table[32 * q : 32 * q + 4, :].bitcast(I32), in_=x_scales[0, 4 * q : 4 * q + 4, :].bitcast(I32))
+        for r in range(4):
+            nc.sync.dma_start(out=scale_table[r:P:32, :].bitcast(I32), in_=x_scales[0, r:16:4, :].bitcast(I32))
 
         w1_rest = load(w1, slice(LEAD, H), "w1_rest")
         word_table = keep.tile([P, T], I32, name="word_table", align_bytes=64)

@@ -13,15 +13,17 @@ U16 = mybir.dt.uint16
 U8 = mybir.dt.uint8
 FP8X4 = mybir.dt.float8_e4m3fn_x4
 ACT = mybir.ActivationFunctionType
+ALU = mybir.AluOpType
 
 P = 128
 PACK = 4
 BANK = 128
-LEAD = 256
+HALF = H // 2
 GATHERS = (256, 256, 512)
+H_PIECES = ((0, 512, "w2_raw"), (512, 256, "h_middle"), (768, 256, "r1_grouped"))
 STRETCHES = ((0, 256), (256, 256), (512, 256), (768, 128), (896, 128))
 STORE_ENDS = (256, 512, 896, 1024)
-H_VECTOR_BANKS = {7: 64}
+H_VECTOR_BANKS = {7: 96}
 G_VECTOR_BANKS = {0: 0, 2: 0, 3: 0}
 
 
@@ -36,7 +38,7 @@ def tile_picked_yrnd_sq_p_kernel(tc, x_words, x_scales, w1, r1, w2, r2, offs, ou
             nc.sync.dma_start(out=rows[:], in_=w.rearrange("(p j) c -> p j c", j=PACK)[:, :, cols])
             return rows
 
-        w1_lead = load(w1, slice(0, LEAD), "w1_lead")
+        w1_lead = load(w1, slice(0, HALF), "w1_lead")
 
         offsets = keep.tile([P, S // 16], U16, name="offsets")
         nc.sync.dma_start(offsets[:], offs)
@@ -46,13 +48,13 @@ def tile_picked_yrnd_sq_p_kernel(tc, x_words, x_scales, w1, r1, w2, r2, offs, ou
         for r in range(4):
             nc.sync.dma_start(out=scale_table[r:P:32, :].bitcast(I32), in_=x_scales[0, r:16:4, :].bitcast(I32))
 
-        w1_rest = load(w1, slice(LEAD, H), "w1_rest")
+        w1_rest = load(w1, slice(HALF, H), "w1_rest")
         word_table = keep.tile([P, T], I32, name="word_table", align_bytes=64)
         nc.sync.dma_start(out=word_table[:], in_=x_words[0].rearrange("p n t -> p (n t)").bitcast(I32))
         w2_raw = load(w2, slice(0, N), "w2_raw")
         r2_raw = load(r2, slice(0, N), "r2_raw")
-        r1_lead = load(r1, slice(0, LEAD), "r1_lead")
-        r1_rest = load(r1, slice(LEAD, H), "r1_rest")
+        r1_lead = load(r1, slice(0, HALF), "r1_lead")
+        r1_rest = load(r1, slice(HALF, H), "r1_rest")
 
         def quantize(values, width, tag):
             codes = keep.tile([P, width], U32, name=f"{tag}_codes", align_bytes=64)
@@ -60,20 +62,25 @@ def tile_picked_yrnd_sq_p_kernel(tc, x_words, x_scales, w1, r1, w2, r2, offs, ou
             nc.vector.quantize_mx(out=codes[:].bitcast(FP8X4), scales=scales[:], in_=values)
             return codes, scales
 
-        def prepare_first(tag, copies):
-            grouped = keep.tile([P, PACK * H], BF16, name=f"{tag}_grouped", tag=f"{tag}_grouped", align_bytes=64)
-            view = grouped[:].rearrange("p (t m j) -> p m j t", t=PACK, j=PACK)
-            for rows, first, copy in copies:
-                copy(view[:, first // PACK : (first + rows.shape[2]) // PACK, :, :], rows.rearrange("p j (m t) -> p m j t", t=PACK))
-            return quantize(grouped[:], H, tag)
+        def dealt(grouped):
+            return grouped[:].rearrange("p (t m j) -> p m j t", t=PACK, j=PACK)
+
+        def by_group(rows):
+            return rows[:].rearrange("p j (m t) -> p m j t", t=PACK)
 
         def entries(first, width):
             return offsets[:, first // 16 : (first + width) // 16]
 
+        lead_columns = slice(0, HALF // PACK)
+        rest_columns = slice(HALF // PACK, H // PACK)
+
         picked_scales = keep.tile([P, S], U8, name="picked_scales", align_bytes=64)
         nc.vector.tensor_copy(picked_scales[:], scale_table[:].indirect(entries(0, S)))
 
-        w1_q = prepare_first("w1", [(w1_lead[:], 0, nc.scalar.copy), (w1_rest[:], LEAD, nc.scalar.copy)])
+        w1_grouped = keep.tile([P, PACK * H], BF16, name="w1_grouped", tag="w1_grouped", align_bytes=64)
+        nc.scalar.copy(dealt(w1_grouped)[:, lead_columns, :, :], by_group(w1_lead))
+        nc.scalar.copy(dealt(w1_grouped)[:, rest_columns, :, :], by_group(w1_rest))
+        w1_q = quantize(w1_grouped[:], H, "w1")
 
         picked_words = keep.tile([P, S], U32, name="picked_words", tag="w1_rest", align_bytes=64)
         first = 0
@@ -83,13 +90,12 @@ def tile_picked_yrnd_sq_p_kernel(tc, x_words, x_scales, w1, r1, w2, r2, offs, ou
 
         second_grouped = keep.tile([P, 2, N, PACK], BF16, name="second_grouped", align_bytes=64)
         nc.scalar.copy(second_grouped[:, 0, :, :].rearrange("p (c i) j -> p c j i", i=PACK), w2_raw[:].rearrange("p j (c i) -> p c j i", i=PACK))
-        nc.scalar.activation(second_grouped[:, 1, :, :].rearrange("p (c i) j -> p c j i", i=PACK), r2_raw[:].rearrange("p j (c i) -> p c j i", i=PACK), ACT.Copy, scale=-1.0)
+        nc.gpsimd.tensor_scalar(second_grouped[:, 1, :, :], r2_raw[:].rearrange("p j n -> p n j"), -1.0, 0.0, ALU.mult, ALU.add)
 
         r1_grouped = keep.tile([P, PACK * H], BF16, name="r1_grouped", tag="r1_grouped", align_bytes=64)
-        r1_view = r1_grouped[:].rearrange("p (t m j) -> p m j t", t=PACK, j=PACK)
-        nc.vector.tensor_copy(r1_view[:, : LEAD // PACK, :, :], r1_lead[:].rearrange("p j (m t) -> p m j t", t=PACK))
+        nc.vector.tensor_copy(dealt(r1_grouped)[:, lead_columns, :, :], by_group(r1_lead))
         for t in (0, 2):
-            nc.vector.tensor_copy(r1_view[:, LEAD // PACK :, :, t : t + 2], r1_rest[:].rearrange("p j (m t) -> p m j t", t=PACK)[:, :, :, t : t + 2])
+            nc.vector.tensor_copy(dealt(r1_grouped)[:, rest_columns, :, t : t + 2], by_group(r1_rest)[:, :, :, t : t + 2])
         r1_codes = keep.tile([P, H], U32, name="r1_codes", align_bytes=64)
         r1_scales = keep.tile([P, H], U8, name="r1_scales", align_bytes=64)
         for t in (0, 2):
@@ -119,7 +125,7 @@ def tile_picked_yrnd_sq_p_kernel(tc, x_words, x_scales, w1, r1, w2, r2, offs, ou
 
         h_codes = keep.tile([P, S], U32, name="h_codes", tag="r1_rest", align_bytes=64)
         h_scales = keep.tile([P, S], U8, name="h_scales", align_bytes=64)
-        for first, width, slot in ((0, 512, "r2_raw"), (512, 256, "h_middle"), (768, 256, "r1_grouped")):
+        for first, width, slot in H_PIECES:
             h_values = hidden(w1_q, first, width, "h", slot, H_VECTOR_BANKS)
             cols = slice(first, first + width)
             nc.vector.quantize_mx(out=h_codes[:, cols].bitcast(FP8X4), scales=h_scales[:, cols], in_=h_values)
@@ -131,16 +137,22 @@ def tile_picked_yrnd_sq_p_kernel(tc, x_words, x_scales, w1, r1, w2, r2, offs, ou
                 if first <= start < first + S // 2:
                     g_q.append(quantize(g_values[:, PACK * (start - first) : PACK * (start - first + width)], width, f"g{start}"))
 
+        def second_layer(difference, w, codes, scales):
+            rows = slice(w * N, (w + 1) * N)
+            nc.tensor.matmul_mx(out=difference[:], lhsT=second_codes[:, rows].bitcast(FP8X4), lhsT_scale=second_scales[:, rows],
+                                rhs=codes.bitcast(FP8X4), rhs_scale=scales, start=(w == 0), stop=(w == 1))
+
+        differences = []
+        for stretch, (first, width) in enumerate(STRETCHES):
+            differences.append(psum.tile([P, width], F32, name=f"diff{first}", tag=f"bank{stretch}"))
+            second_layer(differences[stretch], 0, h_codes[:, first : first + width], h_scales[:, first : first + width])
+
         result = keep.tile([P, S], F32, name="result")
         stored = 0
-        for (first, width), (g_codes, g_scales) in zip(STRETCHES, g_q):
+        for (first, width), difference, (g_codes, g_scales) in zip(STRETCHES, differences, g_q):
             inside = slice(first, first + width)
-            diff = psum.tile([P, width], F32, name=f"diff{first}", tag=f"bank{first // BANK}")
-            for w, (codes, scales) in enumerate(((h_codes[:, inside], h_scales[:, inside]), (g_codes[:], g_scales[:]))):
-                rows = slice(w * N, (w + 1) * N)
-                nc.tensor.matmul_mx(out=diff[:], lhsT=second_codes[:, rows].bitcast(FP8X4), lhsT_scale=second_scales[:, rows],
-                                    rhs=codes.bitcast(FP8X4), rhs_scale=scales, start=(w == 0), stop=(w == 1))
-            nc.scalar.activation(result[:, inside], diff[:], ACT.Square)
+            second_layer(difference, 1, g_codes[:], g_scales[:])
+            nc.scalar.activation(result[:, inside], difference[:], ACT.Square)
             if inside.stop in STORE_ENDS:
                 nc.sync.dma_start(out=out[:, stored : inside.stop], in_=result[:, stored : inside.stop])
                 stored = inside.stop

@@ -19,7 +19,7 @@ P = 128
 PACK = 4
 BANK = 128
 HALF = H // 2
-GATHERS = (256, 256, 512)
+GATHERS = (128, 128, 256, 512)
 H_PIECES = ((0, 512, "w2_raw"), (512, 256, "h_middle"), (768, 256, "r1_grouped"))
 STRETCHES = ((0, 256), (256, 256), (512, 256), (768, 128), (896, 128))
 STORE_ENDS = (256, 512, 896, 1024)

@@ -19,6 +19,7 @@ P = 128
 PACK = 4
 BANK = 128
 HALF = H // 2
+SCALAR_SHARE = 160
 GATHERS = (128, 128, 256, 512)
 H_PIECES = ((0, 512, "w2_raw"), (512, 256, "h_middle"), (768, 256, "r1_grouped"))
 STRETCHES = ((0, 256), (256, 256), (512, 256), (768, 128), (896, 128))
@@ -46,7 +47,7 @@ def tile_picked_yrnd_sq_p_kernel(tc, x_words, x_scales, w1, r1, w2, r2, offs, ou
         scale_table = keep.tile([P, T], U8, name="scale_table", align_bytes=64)
         nc.vector.memset(scale_table[:].bitcast(I32), 0)
         for r in range(4):
-            nc.sync.dma_start(out=scale_table[r:P:32, :].bitcast(I32), in_=x_scales[0, r:16:4, :].bitcast(I32))
+            nc.scalar.dma_start(out=scale_table[r:P:32, :].bitcast(I32), in_=x_scales[0, r:16:4, :].bitcast(I32))
 
         w1_rest = load(w1, slice(HALF, H), "w1_rest")
         word_table = keep.tile([P, T], I32, name="word_table", align_bytes=64)
@@ -79,7 +80,10 @@ def tile_picked_yrnd_sq_p_kernel(tc, x_words, x_scales, w1, r1, w2, r2, offs, ou
 
         w1_grouped = keep.tile([P, PACK * H], BF16, name="w1_grouped", tag="w1_grouped", align_bytes=64)
         nc.scalar.copy(dealt(w1_grouped)[:, lead_columns, :, :], by_group(w1_lead))
-        nc.scalar.copy(dealt(w1_grouped)[:, rest_columns, :, :], by_group(w1_rest))
+        share = SCALAR_SHARE // PACK
+        nc.scalar.copy(dealt(w1_grouped)[:, HALF // PACK : HALF // PACK + share, :, :], by_group(w1_rest)[:, 0:share, :, :])
+        nc.gpsimd.tensor_scalar(w1_grouped[:].rearrange("p (t m j) -> p m t j", t=PACK, j=PACK)[:, HALF // PACK + share :, :, :],
+                                w1_rest[:].rearrange("p j (m t) -> p m t j", t=PACK)[:, share:, :, :], 1.0, 0.0, ALU.mult, ALU.add)
         w1_q = quantize(w1_grouped[:], H, "w1")
 
         picked_words = keep.tile([P, S], U32, name="picked_words", tag="w1_rest", align_bytes=64)

@@ -47,7 +47,7 @@ def tile_picked_yrnd_sq_p_kernel(tc, x_words, x_scales, w1, r1, w2, r2, offs, ou
         scale_table = keep.tile([P, T], U8, name="scale_table", align_bytes=64)
         nc.vector.memset(scale_table[:].bitcast(I32), 0)
         for r in range(4):
-            nc.scalar.dma_start(out=scale_table[r:P:32, :].bitcast(I32), in_=x_scales[0, r:16:4, :].bitcast(I32))
+            nc.sync.dma_start(out=scale_table[r:P:32, :].bitcast(I32), in_=x_scales[0, r:16:4, :].bitcast(I32))
 
         w1_rest = load(w1, slice(HALF, H), "w1_rest")
         word_table = keep.tile([P, T], I32, name="word_table", align_bytes=64)

@@ -19,7 +19,8 @@ P = 128
 PACK = 4
 BANK = 128
 HALF = H // 2
-SCALAR_SHARE = 160
+LEAD = 128
+SCALAR_SHARE = 256
 GATHERS = (128, 128, 256, 512)
 H_PIECES = ((0, 512, "w2_raw"), (512, 256, "h_middle"), (768, 256, "r1_grouped"))
 STRETCHES = ((0, 256), (256, 256), (512, 256), (768, 128), (896, 128))
@@ -39,7 +40,7 @@ def tile_picked_yrnd_sq_p_kernel(tc, x_words, x_scales, w1, r1, w2, r2, offs, ou
             nc.sync.dma_start(out=rows[:], in_=w.rearrange("(p j) c -> p j c", j=PACK)[:, :, cols])
             return rows
 
-        w1_lead = load(w1, slice(0, HALF), "w1_lead")
+        w1_lead = load(w1, slice(0, LEAD), "w1_lead")
 
         offsets = keep.tile([P, S // 16], U16, name="offsets")
         nc.sync.dma_start(offsets[:], offs)
@@ -49,7 +50,7 @@ def tile_picked_yrnd_sq_p_kernel(tc, x_words, x_scales, w1, r1, w2, r2, offs, ou
         for r in range(4):
             nc.sync.dma_start(out=scale_table[r:P:32, :].bitcast(I32), in_=x_scales[0, r:16:4, :].bitcast(I32))
 
-        w1_rest = load(w1, slice(HALF, H), "w1_rest")
+        w1_rest = load(w1, slice(LEAD, H), "w1_rest")
         word_table = keep.tile([P, T], I32, name="word_table", align_bytes=64)
         nc.sync.dma_start(out=word_table[:], in_=x_words[0].rearrange("p n t -> p (n t)").bitcast(I32))
         w2_raw = load(w2, slice(0, N), "w2_raw")
@@ -79,10 +80,10 @@ def tile_picked_yrnd_sq_p_kernel(tc, x_words, x_scales, w1, r1, w2, r2, offs, ou
         nc.vector.tensor_copy(picked_scales[:], scale_table[:].indirect(entries(0, S)))
 
         w1_grouped = keep.tile([P, PACK * H], BF16, name="w1_grouped", tag="w1_grouped", align_bytes=64)
-        nc.scalar.copy(dealt(w1_grouped)[:, lead_columns, :, :], by_group(w1_lead))
+        nc.scalar.copy(dealt(w1_grouped)[:, 0 : LEAD // PACK, :, :], by_group(w1_lead))
         share = SCALAR_SHARE // PACK
-        nc.scalar.copy(dealt(w1_grouped)[:, HALF // PACK : HALF // PACK + share, :, :], by_group(w1_rest)[:, 0:share, :, :])
-        nc.gpsimd.tensor_scalar(w1_grouped[:].rearrange("p (t m j) -> p m t j", t=PACK, j=PACK)[:, HALF // PACK + share :, :, :],
+        nc.scalar.copy(dealt(w1_grouped)[:, LEAD // PACK : LEAD // PACK + share, :, :], by_group(w1_rest)[:, 0:share, :, :])
+        nc.gpsimd.tensor_scalar(w1_grouped[:].rearrange("p (t m j) -> p m t j", t=PACK, j=PACK)[:, LEAD // PACK + share :, :, :],
                                 w1_rest[:].rearrange("p j (m t) -> p m t j", t=PACK)[:, share:, :, :], 1.0, 0.0, ALU.mult, ALU.add)
         w1_q = quantize(w1_grouped[:], H, "w1")
 

@@ -26,7 +26,7 @@ H_PIECES = ((0, 512, "w2_raw"), (512, 256, "h_middle"), (768, 256, "r1_grouped")
 STRETCHES = ((0, 256), (256, 256), (512, 256), (768, 128), (896, 128))
 STORE_ENDS = (256, 512, 896, 1024)
 H_VECTOR_BANKS = {7: 96}
-G_VECTOR_BANKS = {0: 0, 2: 0, 3: 0}
+G_VECTOR_BANKS = {1: 0, 2: 0, 3: 0}
 
 
 def tile_picked_yrnd_sq_p_kernel(tc, x_words, x_scales, w1, r1, w2, r2, offs, out):

@@ -20,6 +20,7 @@ PACK = 4
 BANK = 128
 HALF = H // 2
 LEAD = 128
+SPREAD = 32
 SCALAR_SHARE = 256
 GATHERS = (128, 128, 256, 512)
 H_PIECES = ((0, 512, "w2_raw"), (512, 256, "h_middle"), (768, 256, "r1_grouped"))
@@ -33,30 +34,59 @@ def tile_picked_yrnd_sq_p_kernel(tc, x_words, x_scales, w1, r1, w2, r2, offs, ou
     nc = tc.nc
     with ExitStack() as ctx:
         keep = ctx.enter_context(tc.tile_pool(name="keep", bufs=1))
+        shared = ctx.enter_context(tc.tile_pool(name="shared", bufs=1))
         psum = ctx.enter_context(tc.psum_pool(name="psum", bufs=1))
 
-        def load(w, cols, name):
-            rows = keep.tile([P, PACK, cols.stop - cols.start], F32, name=name, tag=name, align_bytes=64)
-            nc.sync.dma_start(out=rows[:], in_=w.rearrange("(p j) c -> p j c", j=PACK)[:, :, cols])
+        def placed(name, shape, dtype, byte):
+            return shared.tile(shape, dtype, name=name, offset=byte, align_bytes=64)
+
+        def load_into(rows, w, cols):
+            nc.sync.dma_start(out=rows, in_=w.rearrange("(p j) c -> p j c", j=PACK)[:, :, cols])
             return rows
 
-        w1_lead = load(w1, slice(0, LEAD), "w1_lead")
+        def load(w, cols, name):
+            return load_into(keep.tile([P, PACK, cols.stop - cols.start], F32, name=name, tag=name, align_bytes=64)[:], w, cols)
+
+        w1_lead = load_into(placed("w1_lead", [P, PACK, LEAD], F32, 4608)[:], w1, slice(0, LEAD))
 
         offsets = keep.tile([P, S // 16], U16, name="offsets")
         nc.sync.dma_start(offsets[:], offs)
 
-        scale_table = keep.tile([P, T], U8, name="scale_table", align_bytes=64)
+        scale_table = keep.tile([P, T], U8, name="scale_table", tag="scale_table", align_bytes=64)
         nc.vector.memset(scale_table[:].bitcast(I32), 0)
-        for r in range(4):
-            nc.sync.dma_start(out=scale_table[r:P:32, :].bitcast(I32), in_=x_scales[0, r:16:4, :].bitcast(I32))
+        nc.sync.dma_start(out=scale_table[SPREAD : SPREAD + 64 : 4, :].bitcast(I32), in_=x_scales[0].bitcast(I32))
 
         w1_rest = load(w1, slice(LEAD, H), "w1_rest")
         word_table = keep.tile([P, T], I32, name="word_table", align_bytes=64)
         nc.sync.dma_start(out=word_table[:], in_=x_words[0].rearrange("p n t -> p (n t)").bitcast(I32))
-        w2_raw = load(w2, slice(0, N), "w2_raw")
-        r2_raw = load(r2, slice(0, N), "r2_raw")
-        r1_lead = load(r1, slice(0, HALF), "r1_lead")
-        r1_rest = load(r1, slice(HALF, H), "r1_rest")
+
+        def dealt(grouped):
+            return grouped[:].rearrange("p (t m j) -> p m j t", t=PACK, j=PACK)
+
+        def by_group(rows):
+            return rows.rearrange("p j (m t) -> p m j t", t=PACK)
+
+        w1_grouped = keep.tile([P, PACK * H], BF16, name="w1_grouped", tag="w1_grouped", align_bytes=64)
+        nc.scalar.copy(dealt(w1_grouped)[:, 0 : LEAD // PACK, :, :], by_group(w1_lead))
+
+        def entries(first, width):
+            return offsets[:, first // 16 : (first + width) // 16]
+
+        picked_scales = keep.tile([P, S], U8, name="picked_scales", align_bytes=64)
+        nc.vector.memset(picked_scales[:].bitcast(I32), 0)
+
+        def pick_scales(spread, first):
+            nc.vector.tensor_copy(spread[:], scale_table[:].indirect(entries(first, S // 2)))
+            for r in range(4):
+                nc.sync.dma_start(out=picked_scales[r:P:32, first : first + S // 2].bitcast(I32), in_=spread[SPREAD + 4 * r : SPREAD + 64 : 16, :].bitcast(I32))
+
+        pick_scales(keep.tile([P, S // 2], U8, name="spread_first", align_bytes=64), 0)
+        w2_raw = load_into(placed("w2_raw", [P, PACK, N], F32, 3072)[:], w2, slice(0, N))
+        middle = placed("middle", [P, PACK * (N + HALF)], F32, 6144)
+        r2_raw = load_into(middle[:, : PACK * N].rearrange("p (j c) -> p j c", j=PACK), r2, slice(0, N))
+        r1_lead = load_into(middle[:, PACK * N :].rearrange("p (j c) -> p j c", j=PACK), r1, slice(0, HALF))
+        pick_scales(placed("spread_second", [P, S // 2], U8, 5376), S // 2)
+        r1_rest = load_into(keep.tile([P, PACK, HALF], F32, name="r1_rest", tag="scale_table", align_bytes=64)[:], r1, slice(HALF, H))
 
         def quantize(values, width, tag):
             codes = keep.tile([P, width], U32, name=f"{tag}_codes", align_bytes=64)
@@ -64,27 +94,13 @@ def tile_picked_yrnd_sq_p_kernel(tc, x_words, x_scales, w1, r1, w2, r2, offs, ou
             nc.vector.quantize_mx(out=codes[:].bitcast(FP8X4), scales=scales[:], in_=values)
             return codes, scales
 
-        def dealt(grouped):
-            return grouped[:].rearrange("p (t m j) -> p m j t", t=PACK, j=PACK)
-
-        def by_group(rows):
-            return rows[:].rearrange("p j (m t) -> p m j t", t=PACK)
-
-        def entries(first, width):
-            return offsets[:, first // 16 : (first + width) // 16]
-
         lead_columns = slice(0, HALF // PACK)
         rest_columns = slice(HALF // PACK, H // PACK)
 
-        picked_scales = keep.tile([P, S], U8, name="picked_scales", align_bytes=64)
-        nc.vector.tensor_copy(picked_scales[:], scale_table[:].indirect(entries(0, S)))
-
-        w1_grouped = keep.tile([P, PACK * H], BF16, name="w1_grouped", tag="w1_grouped", align_bytes=64)
-        nc.scalar.copy(dealt(w1_grouped)[:, 0 : LEAD // PACK, :, :], by_group(w1_lead))
         share = SCALAR_SHARE // PACK
         nc.scalar.copy(dealt(w1_grouped)[:, LEAD // PACK : LEAD // PACK + share, :, :], by_group(w1_rest)[:, 0:share, :, :])
         nc.gpsimd.tensor_scalar(w1_grouped[:].rearrange("p (t m j) -> p m t j", t=PACK, j=PACK)[:, LEAD // PACK + share :, :, :],
-                                w1_rest[:].rearrange("p j (m t) -> p m t j", t=PACK)[:, share:, :, :], 1.0, 0.0, ALU.mult, ALU.add)
+                                w1_rest.rearrange("p j (m t) -> p m t j", t=PACK)[:, share:, :, :], 1.0, 0.0, ALU.mult, ALU.add)
         w1_q = quantize(w1_grouped[:], H, "w1")
 
         picked_words = keep.tile([P, S], U32, name="picked_words", tag="w1_rest", align_bytes=64)
@@ -94,8 +110,8 @@ def tile_picked_yrnd_sq_p_kernel(tc, x_words, x_scales, w1, r1, w2, r2, offs, ou
             first = first + width
 
         second_grouped = keep.tile([P, 2, N, PACK], BF16, name="second_grouped", align_bytes=64)
-        nc.scalar.copy(second_grouped[:, 0, :, :].rearrange("p (c i) j -> p c j i", i=PACK), w2_raw[:].rearrange("p j (c i) -> p c j i", i=PACK))
-        nc.gpsimd.tensor_scalar(second_grouped[:, 1, :, :], r2_raw[:].rearrange("p j n -> p n j"), -1.0, 0.0, ALU.mult, ALU.add)
+        nc.scalar.copy(second_grouped[:, 0, :, :].rearrange("p (c i) j -> p c j i", i=PACK), w2_raw.rearrange("p j (c i) -> p c j i", i=PACK))
+        nc.gpsimd.tensor_scalar(second_grouped[:, 1, :, :], r2_raw.rearrange("p j n -> p n j"), -1.0, 0.0, ALU.mult, ALU.add)
 
         r1_grouped = keep.tile([P, PACK * H], BF16, name="r1_grouped", tag="r1_grouped", align_bytes=64)
         nc.vector.tensor_copy(dealt(r1_grouped)[:, lead_columns, :, :], by_group(r1_lead))
@@ -111,7 +127,10 @@ def tile_picked_yrnd_sq_p_kernel(tc, x_words, x_scales, w1, r1, w2, r2, offs, ou
 
         def hidden(weights, first, width, tag, slot, vector_banks):
             codes, scales = weights
-            values = keep.tile([P, width, PACK], BF16, name=f"{tag}_values{first}", tag=slot, align_bytes=64)
+            if slot == "w2_raw":
+                values = placed("h_values0", [P, width, PACK], BF16, 0)
+            else:
+                values = keep.tile([P, width, PACK], BF16, name=f"{tag}_values{first}", tag=slot, align_bytes=64)
             for b in range(first // BANK, (first + width) // BANK):
                 cols = slice(b * BANK, (b + 1) * BANK)
                 acc = psum.tile([P, PACK, BANK], F32, name=f"{tag}_acc{b}", tag=f"bank{b}")
@@ -128,7 +147,7 @@ def tile_picked_yrnd_sq_p_kernel(tc, x_words, x_scales, w1, r1, w2, r2, offs, ou
                     nc.scalar.activation(target[:, :split, :], stepped[:, :split, :], ACT.Relu)
             return values[:].rearrange("p n t -> p (n t)")
 
-        h_codes = keep.tile([P, S], U32, name="h_codes", tag="r1_rest", align_bytes=64)
+        h_codes = keep.tile([P, S], U32, name="h_codes", tag="scale_table", align_bytes=64)
         h_scales = keep.tile([P, S], U8, name="h_scales", align_bytes=64)
         for first, width, slot in H_PIECES:
             h_values = hidden(w1_q, first, width, "h", slot, H_VECTOR_BANKS)

@@ -20,7 +20,7 @@ PACK = 4
 BANK = 128
 HALF = H // 2
 LEAD = 128
-SPREAD = 32
+SPREAD = 8
 SCALAR_SHARE = 256
 GATHERS = (128, 128, 256, 512)
 H_PIECES = ((0, 512, "w2_raw"), (512, 256, "h_middle"), (768, 256, "r1_grouped"))
@@ -54,7 +54,7 @@ def tile_picked_yrnd_sq_p_kernel(tc, x_words, x_scales, w1, r1, w2, r2, offs, ou
 
         scale_table = keep.tile([P, T], U8, name="scale_table", tag="scale_table", align_bytes=64)
         nc.vector.memset(scale_table[:].bitcast(I32), 0)
-        nc.sync.dma_start(out=scale_table[SPREAD : SPREAD + 64 : 4, :].bitcast(I32), in_=x_scales[0].bitcast(I32))
+        nc.sync.dma_start(out=scale_table[0:P:SPREAD, :].bitcast(I32), in_=x_scales[0].bitcast(I32))
 
         w1_rest = load(w1, slice(LEAD, H), "w1_rest")
         word_table = keep.tile([P, T], I32, name="word_table", align_bytes=64)
@@ -73,12 +73,12 @@ def tile_picked_yrnd_sq_p_kernel(tc, x_words, x_scales, w1, r1, w2, r2, offs, ou
             return offsets[:, first // 16 : (first + width) // 16]
 
         picked_scales = keep.tile([P, S], U8, name="picked_scales", align_bytes=64)
-        nc.vector.memset(picked_scales[:].bitcast(I32), 0)
 
         def pick_scales(spread, first):
             nc.vector.tensor_copy(spread[:], scale_table[:].indirect(entries(first, S // 2)))
-            for r in range(4):
-                nc.sync.dma_start(out=picked_scales[r:P:32, first : first + S // 2].bitcast(I32), in_=spread[SPREAD + 4 * r : SPREAD + 64 : 16, :].bitcast(I32))
+            nc.vector.tensor_copy(picked_scales[:, first : first + S // 2].bitcast(I32), spread[:].bitcast(I32))
+            for r in range(1, 4):
+                nc.sync.dma_start(out=picked_scales[r:P:32, first : first + S // 2].bitcast(I32), in_=spread[SPREAD * r : P : 32, :].bitcast(I32))
 
         pick_scales(keep.tile([P, S // 2], U8, name="spread_first", align_bytes=64), 0)
         w2_raw = load_into(placed("w2_raw", [P, PACK, N], F32, 3072)[:], w2, slice(0, N))

@@ -20,6 +20,7 @@ PACK = 4
 BANK = 128
 HALF = H // 2
 LEAD = 128
+EARLY = 384
 SPREAD = 8
 SCALAR_SHARE = 256
 GATHERS = (128, 128, 256, 512)
@@ -74,18 +75,18 @@ def tile_picked_yrnd_sq_p_kernel(tc, x_words, x_scales, w1, r1, w2, r2, offs, ou
 
         picked_scales = keep.tile([P, S], U8, name="picked_scales", align_bytes=64)
 
-        def pick_scales(spread, first):
-            nc.vector.tensor_copy(spread[:], scale_table[:].indirect(entries(first, S // 2)))
-            nc.vector.tensor_copy(picked_scales[:, first : first + S // 2].bitcast(I32), spread[:].bitcast(I32))
+        def pick_scales(spread, first, width):
+            nc.vector.tensor_copy(spread[:], scale_table[:].indirect(entries(first, width)))
+            nc.vector.tensor_copy(picked_scales[:, first : first + width].bitcast(I32), spread[:].bitcast(I32))
             for r in range(1, 4):
-                nc.sync.dma_start(out=picked_scales[r:P:32, first : first + S // 2].bitcast(I32), in_=spread[SPREAD * r : P : 32, :].bitcast(I32))
+                nc.sync.dma_start(out=picked_scales[r:P:32, first : first + width].bitcast(I32), in_=spread[SPREAD * r : P : 32, :].bitcast(I32))
 
-        pick_scales(keep.tile([P, S // 2], U8, name="spread_first", align_bytes=64), 0)
+        pick_scales(keep.tile([P, EARLY], U8, name="spread_first", align_bytes=64), 0, EARLY)
         w2_raw = load_into(placed("w2_raw", [P, PACK, N], F32, 3072)[:], w2, slice(0, N))
         middle = placed("middle", [P, PACK * (N + HALF)], F32, 6144)
         r2_raw = load_into(middle[:, : PACK * N].rearrange("p (j c) -> p j c", j=PACK), r2, slice(0, N))
         r1_lead = load_into(middle[:, PACK * N :].rearrange("p (j c) -> p j c", j=PACK), r1, slice(0, HALF))
-        pick_scales(placed("spread_second", [P, S // 2], U8, 5376), S // 2)
+        pick_scales(placed("spread_second", [P, S - EARLY], U8, 5376), EARLY, S - EARLY)
         r1_rest = load_into(keep.tile([P, PACK, HALF], F32, name="r1_rest", tag="scale_table", align_bytes=64)[:], r1, slice(HALF, H))
 
         def quantize(values, width, tag):

from contextlib import ExitStack

import concourse.mybir as mybir

K, T, S, H, N = 512, 2048, 1024, 512, 128
FLOPS = 2 * 2 * S * (K * H + H * N)

F32 = mybir.dt.float32
BF16 = mybir.dt.bfloat16
I32 = mybir.dt.int32
U32 = mybir.dt.uint32
U16 = mybir.dt.uint16
U8 = mybir.dt.uint8
FP8X4 = mybir.dt.float8_e4m3fn_x4
ACT = mybir.ActivationFunctionType
ALU = mybir.AluOpType

P = 128
PACK = 4
BANK = 128
HALF = H // 2
LEAD = 128
EARLY = 384
SPREAD = 8
SCALAR_SHARE = 256
GATHERS = (128, 128, 256, 512)
H_PIECES = ((0, 512, "w2_raw"), (512, 256, "h_middle"), (768, 256, "r1_grouped"))
STRETCHES = ((0, 256), (256, 256), (512, 256), (768, 128), (896, 128))
STORE_ENDS = (256, 512, 896, 1024)
H_VECTOR_BANKS = {7: 96}
G_VECTOR_BANKS = {1: 0, 2: 0, 3: 0}


def tile_picked_yrnd_sq_p_kernel(tc, x_words, x_scales, w1, r1, w2, r2, offs, out):
    nc = tc.nc
    with ExitStack() as ctx:
        keep = ctx.enter_context(tc.tile_pool(name="keep", bufs=1))
        shared = ctx.enter_context(tc.tile_pool(name="shared", bufs=1))
        psum = ctx.enter_context(tc.psum_pool(name="psum", bufs=1))

        def placed(name, shape, dtype, byte):
            return shared.tile(shape, dtype, name=name, offset=byte, align_bytes=64)

        def load_into(rows, w, cols):
            nc.sync.dma_start(out=rows, in_=w.rearrange("(p j) c -> p j c", j=PACK)[:, :, cols])
            return rows

        def load(w, cols, name):
            return load_into(keep.tile([P, PACK, cols.stop - cols.start], F32, name=name, tag=name, align_bytes=64)[:], w, cols)

        w1_lead = load_into(placed("w1_lead", [P, PACK, LEAD], F32, 4608)[:], w1, slice(0, LEAD))

        offsets = keep.tile([P, S // 16], U16, name="offsets")
        nc.sync.dma_start(offsets[:], offs)

        scale_table = keep.tile([P, T], U8, name="scale_table", tag="scale_table", align_bytes=64)
        nc.vector.memset(scale_table[:].bitcast(I32), 0)
        nc.sync.dma_start(out=scale_table[0:P:SPREAD, :].bitcast(I32), in_=x_scales[0].bitcast(I32))

        w1_rest = load(w1, slice(LEAD, H), "w1_rest")
        word_table = keep.tile([P, T], I32, name="word_table", align_bytes=64)
        nc.sync.dma_start(out=word_table[:], in_=x_words[0].rearrange("p n t -> p (n t)").bitcast(I32))

        def dealt(grouped):
            return grouped[:].rearrange("p (t m j) -> p m j t", t=PACK, j=PACK)

        def by_group(rows):
            return rows.rearrange("p j (m t) -> p m j t", t=PACK)

        w1_grouped = keep.tile([P, PACK * H], BF16, name="w1_grouped", tag="w1_grouped", align_bytes=64)
        nc.scalar.copy(dealt(w1_grouped)[:, 0 : LEAD // PACK, :, :], by_group(w1_lead))

        def entries(first, width):
            return offsets[:, first // 16 : (first + width) // 16]

        picked_scales = keep.tile([P, S], U8, name="picked_scales", align_bytes=64)

        def pick_scales(spread, first, width):
            nc.vector.tensor_copy(spread[:], scale_table[:].indirect(entries(first, width)))
            nc.vector.tensor_copy(picked_scales[:, first : first + width].bitcast(I32), spread[:].bitcast(I32))
            for r in range(1, 4):
                nc.sync.dma_start(out=picked_scales[r:P:32, first : first + width].bitcast(I32), in_=spread[SPREAD * r : P : 32, :].bitcast(I32))

        pick_scales(keep.tile([P, EARLY], U8, name="spread_first", align_bytes=64), 0, EARLY)
        w2_raw = load_into(placed("w2_raw", [P, PACK, N], F32, 3072)[:], w2, slice(0, N))
        middle = placed("middle", [P, PACK * (N + HALF)], F32, 6144)
        r2_raw = load_into(middle[:, : PACK * N].rearrange("p (j c) -> p j c", j=PACK), r2, slice(0, N))
        r1_lead = load_into(middle[:, PACK * N :].rearrange("p (j c) -> p j c", j=PACK), r1, slice(0, HALF))
        pick_scales(placed("spread_second", [P, S - EARLY], U8, 5376), EARLY, S - EARLY)
        r1_rest = load_into(keep.tile([P, PACK, HALF], F32, name="r1_rest", tag="scale_table", align_bytes=64)[:], r1, slice(HALF, H))

        def quantize(values, width, tag):
            codes = keep.tile([P, width], U32, name=f"{tag}_codes", align_bytes=64)
            scales = keep.tile([P, width], U8, name=f"{tag}_scales", align_bytes=64)
            nc.vector.quantize_mx(out=codes[:].bitcast(FP8X4), scales=scales[:], in_=values)
            return codes, scales

        lead_columns = slice(0, HALF // PACK)
        rest_columns = slice(HALF // PACK, H // PACK)

        share = SCALAR_SHARE // PACK
        nc.scalar.copy(dealt(w1_grouped)[:, LEAD // PACK : LEAD // PACK + share, :, :], by_group(w1_rest)[:, 0:share, :, :])
        nc.gpsimd.tensor_scalar(w1_grouped[:].rearrange("p (t m j) -> p m t j", t=PACK, j=PACK)[:, LEAD // PACK + share :, :, :],
                                w1_rest.rearrange("p j (m t) -> p m t j", t=PACK)[:, share:, :, :], 1.0, 0.0, ALU.mult, ALU.add)
        w1_q = quantize(w1_grouped[:], H, "w1")

        picked_words = keep.tile([P, S], U32, name="picked_words", tag="w1_rest", align_bytes=64)
        first = 0
        for width in GATHERS:
            nc.vector.tensor_copy(picked_words[:, first : first + width], word_table[:].bitcast(U32).indirect(entries(first, width)))
            first = first + width

        second_grouped = keep.tile([P, 2, N, PACK], BF16, name="second_grouped", align_bytes=64)
        nc.scalar.copy(second_grouped[:, 0, :, :].rearrange("p (c i) j -> p c j i", i=PACK), w2_raw.rearrange("p j (c i) -> p c j i", i=PACK))
        nc.gpsimd.tensor_scalar(second_grouped[:, 1, :, :], r2_raw.rearrange("p j n -> p n j"), -1.0, 0.0, ALU.mult, ALU.add)

        r1_grouped = keep.tile([P, PACK * H], BF16, name="r1_grouped", tag="r1_grouped", align_bytes=64)
        nc.vector.tensor_copy(dealt(r1_grouped)[:, lead_columns, :, :], by_group(r1_lead))
        for t in (0, 2):
            nc.vector.tensor_copy(dealt(r1_grouped)[:, rest_columns, :, t : t + 2], by_group(r1_rest)[:, :, :, t : t + 2])
        r1_codes = keep.tile([P, H], U32, name="r1_codes", align_bytes=64)
        r1_scales = keep.tile([P, H], U8, name="r1_scales", align_bytes=64)
        for t in (0, 2):
            cols = slice(t * P, (t + 2) * P)
            nc.vector.quantize_mx(out=r1_codes[:, cols].bitcast(FP8X4), scales=r1_scales[:, cols], in_=r1_grouped[:, PACK * cols.start : PACK * cols.stop])
        r1_q = (r1_codes, r1_scales)
        second_codes, second_scales = quantize(second_grouped[:].rearrange("p w n j -> p (w n j)"), 2 * N, "second")

        def hidden(weights, first, width, tag, slot, vector_banks):
            codes, scales = weights
            if slot == "w2_raw":
                values = placed("h_values0", [P, width, PACK], BF16, 0)
            else:
                values = keep.tile([P, width, PACK], BF16, name=f"{tag}_values{first}", tag=slot, align_bytes=64)
            for b in range(first // BANK, (first + width) // BANK):
                cols = slice(b * BANK, (b + 1) * BANK)
                acc = psum.tile([P, PACK, BANK], F32, name=f"{tag}_acc{b}", tag=f"bank{b}")
                for t in range(PACK):
                    group = slice(t * P, (t + 1) * P)
                    nc.tensor.matmul_mx(out=acc[:, t, :], lhsT=codes[:, group].bitcast(FP8X4), lhsT_scale=scales[:, group],
                                        rhs=picked_words[:, cols].bitcast(FP8X4), rhs_scale=picked_scales[:, cols], start=True, stop=True)
                stepped = acc[:].rearrange("p t n -> p n t")
                target = values[:, cols.start - first : cols.stop - first, :]
                split = vector_banks.get(b, BANK)
                if split < BANK:
                    nc.vector.tensor_scalar_max(target[:, split:, :], stepped[:, split:, :], 0.0)
                if split > 0:
                    nc.scalar.activation(target[:, :split, :], stepped[:, :split, :], ACT.Relu)
            return values[:].rearrange("p n t -> p (n t)")

        h_codes = keep.tile([P, S], U32, name="h_codes", tag="scale_table", align_bytes=64)
        h_scales = keep.tile([P, S], U8, name="h_scales", align_bytes=64)
        for first, width, slot in H_PIECES:
            h_values = hidden(w1_q, first, width, "h", slot, H_VECTOR_BANKS)
            cols = slice(first, first + width)
            nc.vector.quantize_mx(out=h_codes[:, cols].bitcast(FP8X4), scales=h_scales[:, cols], in_=h_values)

        g_q = []
        for first in (0, S // 2):
            g_values = hidden(r1_q, first, S // 2, "g", f"g_values{first}", G_VECTOR_BANKS)
            for start, width in STRETCHES:
                if first <= start < first + S // 2:
                    g_q.append(quantize(g_values[:, PACK * (start - first) : PACK * (start - first + width)], width, f"g{start}"))

        def second_layer(difference, w, codes, scales):
            rows = slice(w * N, (w + 1) * N)
            nc.tensor.matmul_mx(out=difference[:], lhsT=second_codes[:, rows].bitcast(FP8X4), lhsT_scale=second_scales[:, rows],
                                rhs=codes.bitcast(FP8X4), rhs_scale=scales, start=(w == 0), stop=(w == 1))

        differences = []
        for stretch, (first, width) in enumerate(STRETCHES):
            differences.append(psum.tile([P, width], F32, name=f"diff{first}", tag=f"bank{stretch}"))
            second_layer(differences[stretch], 0, h_codes[:, first : first + width], h_scales[:, first : first + width])

        result = keep.tile([P, S], F32, name="result")
        stored = 0
        for (first, width), difference, (g_codes, g_scales) in zip(STRETCHES, differences, g_q):
            inside = slice(first, first + width)
            second_layer(difference, 1, g_codes[:], g_scales[:])
            nc.scalar.activation(result[:, inside], difference[:], ACT.Square)
            if inside.stop in STORE_ENDS:
                nc.sync.dma_start(out=out[:, stored : inside.stop], in_=result[:, stored : inside.stop])
                stored = inside.stop
